import numpy as np
import ml_dtypes


def mxq(x, axis, fmt="e4m3"):
    dtype, down = {"e4m3": (ml_dtypes.float8_e4m3fn, 7), "e5m2": (ml_dtypes.float8_e5m2, 14)}[fmt]
    v = np.moveaxis(np.asarray(x, np.float32).astype(ml_dtypes.bfloat16).astype(np.float64), axis, -1)
    blocks = v.reshape(v.shape[:-1] + (-1, 32))
    amax = np.abs(blocks).max(-1, keepdims=True)
    byte = np.maximum(np.where(amax > 0, np.frexp(amax)[1] - 1 + 127, 0) - down, 1)
    scale = np.exp2(byte - 127.0)
    codes = (blocks / scale).astype(np.float32).astype(dtype).astype(np.float64)
    return np.moveaxis((codes * scale).reshape(v.shape), -1, axis)


WIDE = False


def mx_kscale(k):
    if not WIDE:
        return np.ones(k)
    levels = np.array([10, -10, 5, -5, 0])
    if k % 512:
        return np.exp2(np.random.permutation(np.resize(levels, k // 32))).repeat(32)
    a = np.empty((k // 512, 16))
    for p in range(k // 512):
        a[p, :8] = np.random.permutation(np.resize(levels, 8))
        for g in range(8):
            far = levels[np.abs(levels - a[p, g]) >= 10]
            a[p, g + 8] = far[np.random.randint(len(far))]
    return np.exp2(a.ravel()).repeat(32)


BF16 = ml_dtypes.bfloat16


def bf(x):
    return np.asarray(x, np.float32).astype(BF16)


def f64(x):
    return np.asarray(x).astype(np.float64)

def planes(Y):
    n, m = Y.shape
    b = f64(bf(Y)).reshape(n // 32, 32, m)
    amax = np.abs(b).max(1)
    byte = np.clip(np.where(amax > 0, np.frexp(amax)[1] - 1 + 127 - 7, 1), 1, 254)
    codes = (b * np.exp2(127.0 - byte)[:, None, :]).reshape(n, m).astype(np.float32).astype(ml_dtypes.float8_e4m3fn).view(np.uint8)
    words = codes.reshape(n // 512, 128, 4, m).transpose(0, 1, 3, 2)
    return np.ascontiguousarray(words), np.ascontiguousarray(byte.astype(np.uint8).reshape(n // 512, 16, m))


N, M, L = 1024, 512, 1024


def setup_inputs():
    u, t = mx_kscale(M), mx_kscale(L)
    return {"s": bf(3.0 / np.sqrt(L) * np.random.standard_normal((N, L))),
            "z": bf(2.0 / np.sqrt(L) * np.random.standard_normal((M, L)) / u[:, None]),
            "kgain": bf(1.5 / np.sqrt(M) * np.random.standard_normal((N, M)) * u[None, :]),
            "g": bf((1.0 + 0.2 * np.random.standard_normal(L)) * t),
            "d": bf(np.random.uniform(0.5, 2.0, L) / (t * t)),
            "r": bf(np.random.uniform(1.0, 3.0, M) / (u * u))}


def weighted_gram(left, right):
    return left @ right.T


def core(s, z, kgain, g, d, r):
    k = f64(kgain)
    kq = mxq(k, 1, "e4m3")
    kz = kq @ mxq(f64(z), 0, "e4m3")
    w = (f64(s) - kz) * f64(g)[None, :]
    wd = w * f64(d)[None, :]
    j = weighted_gram(mxq(wd, 1, "e4m3"), mxq(w, 1, "e4m3"))
    kr = k * f64(r)[None, :]
    q = weighted_gram(mxq(kr, 1, "e4m3"), kq)
    return j + q


def reference(s, z, kgain, g, d, r):
    R_out = core(s, z, kgain, g, d, r)
    words, scales = planes(R_out.T)
    return R_out, words, scales

@@ -1,0 +1,386 @@
+from contextlib import ExitStack
+
+import concourse.mybir as mybir
+from concourse.masks import make_identity
+
+N, M, L = 1024, 512, 1024
+FLOPS = 2 * N * M * L + 2 * N * L * N + 2 * N * M * N
+
+F32 = mybir.dt.float32
+BF16 = mybir.dt.bfloat16
+U32 = mybir.dt.uint32
+I32 = mybir.dt.int32
+U8 = mybir.dt.uint8
+FP8X4 = mybir.dt.float8_e4m3fn_x4
+MULT = mybir.AluOpType.mult
+SUB = mybir.AluOpType.subtract
+ADD = mybir.AluOpType.add
+COPY = mybir.ActivationFunctionType.Copy
+
+P = 128
+HALF = 512
+CHUNK = 256
+STEPS = 16
+Z_VECTOR_COLS = (352, 0)
+PE_SUM_STEPS = ()
+CAST_ON_GPSIMD = False
+
+
+def tile_josephkalmanupdate_x1_kernel(tc, s, z, kgain, g, d, r, out_0, out_1, out_2):
+    nc = tc.nc
+    words_out = out_1.rearrange("h p m t -> h p (m t)").bitcast(I32)
+    scales_out = out_2.bitcast(I32)
+
+    with ExitStack() as ctx:
+        keep = ctx.enter_context(tc.tile_pool(name="keep", bufs=1))
+        work = ctx.enter_context(tc.tile_pool(name="work", bufs=3))
+        psum = ctx.enter_context(tc.psum_pool(name="psum", bufs=1))
+        ctx.enter_context(tc.manual_schedule())
+
+        def bank(number):
+            return psum.tile([P, HALF], F32, name="bank%d" % number, tag="bank%d" % number)
+
+        def kept(name, shape, dtype):
+            return keep.tile(shape, dtype, name=name, tag=name, align_bytes=64)
+
+        def rotating(name, shape, dtype, bufs):
+            return work.tile(shape, dtype, name=name, tag=name, bufs=bufs, align_bytes=64)
+
+        def quantize(codes, scales, values):
+            nc.vector.quantize_mx(out=codes.bitcast(FP8X4), scales=scales, in_=values)
+
+        def mx(acc, lhs, lhs_cols, rhs, rhs_cols, start, stop):
+            nc.tensor.matmul_mx(
+                out=acc,
+                lhsT=lhs[0][:, lhs_cols].bitcast(FP8X4),
+                lhsT_scale=lhs[1][:, lhs_cols],
+                rhs=rhs[0][:, rhs_cols].bitcast(FP8X4),
+                rhs_scale=rhs[1][:, rhs_cols],
+                start=start,
+                stop=stop,
+            )
+
+        def operand(name):
+            return (kept(name + "_codes", [P, N], U32), kept(name + "_scales", [P, N], U8))
+
+        g_sb = kept("g_sb", [P, 2, 4], BF16)
+        d_sb = kept("d_sb", [P, 2, 4], BF16)
+        r_sb = kept("r_sb", [P, 4], BF16)
+        k_raw = [kept("k_raw%d" % c, [P, 2, M], BF16) for c in range(4)]
+        s_raw = [kept("s_raw%d" % c, [P, 2, L], BF16) for c in range(4)]
+        z_raw = [kept("z_raw%d" % h, [P, 4, HALF], BF16) for h in range(2)]
+
+        def load_k(c):
+            nc.sync.dma_start(out=k_raw[c][:], in_=kgain[c * CHUNK : (c + 1) * CHUNK, :].rearrange("(e p) m -> p e m", p=P))
+
+        def load_s(c):
+            nc.sync.dma_start(out=s_raw[c][:], in_=s[c * CHUNK : (c + 1) * CHUNK, :].rearrange("(e p) l -> p e l", p=P))
+
+        def load_z(h):
+            nc.sync.dma_start(out=z_raw[h][:], in_=z[:, h * HALF : (h + 1) * HALF].rearrange("(p j) l -> p j l", j=4))
+
+        load_k(0)
+        load_z(0)
+        nc.scalar.dma_start(out=r_sb[:], in_=r.rearrange("(p t) -> p t", t=4))
+        nc.scalar.dma_start(out=g_sb[:], in_=g.rearrange("(h p t) -> p h t", h=2, t=4))
+        nc.scalar.dma_start(out=d_sb[:], in_=d.rearrange("(h p t) -> p h t", h=2, t=4))
+        load_s(0)
+        load_z(1)
+        for c in range(1, 4):
+            load_k(c)
+            load_s(c)
+
+        ident = kept("ident", [P, P], F32)
+        make_identity(nc, ident[:])
+
+        kq, krq, zq = operand("kq"), operand("krq"), operand("zq")
+        wq = [operand("wq%d" % h) for h in range(2)]
+        wdq = [operand("wdq%d" % h) for h in range(2)]
+        factors = kept("factors", [P, 2, 2, 4], F32)
+        plane_scales = [kept("plane_scales%d" % h, [P, N], U8) for h in range(2)]
+        k_words = [kept("k_words%d" % c, [P, HALF], F32) for c in range(4)]
+        kr_values = [kept("kr_values%d" % c, [P, 4 * CHUNK], BF16) for c in range(4)]
+        z_grouped = [kept("z_grouped%d" % h, [P, HALF, 4], BF16) for h in range(2)]
+        live = {}
+
+        def chunk_cols(c):
+            return slice(c * CHUNK, (c + 1) * CHUNK)
+
+        def tile_cols(i):
+            return slice(i * P, (i + 1) * P)
+
+        def k_transpose(c, number):
+            acc = bank(number)
+            for e in range(2):
+                words = k_raw[c][:, e, :].bitcast(F32)
+                for u in range(2):
+                    nc.tensor.transpose(acc[:, tile_cols(2 * e + u)], words[:, u::2], ident[:])
+            nc.scalar.copy(
+                out=k_words[c][:].rearrange("p (e n u) -> p e n u", e=2, u=2),
+                in_=acc[:].rearrange("p (e u n) -> p e n u", e=2, u=2),
+            )
+
+        def k_quantize(c):
+            quantize(kq[0][:, chunk_cols(c)], kq[1][:, chunk_cols(c)], k_words[c][:].bitcast(BF16))
+
+        def kr_multiply(c):
+            nc.vector.tensor_tensor(
+                out=kr_values[c][:].rearrange("p (n t) -> p n t", t=4),
+                in0=k_words[c][:].bitcast(BF16).rearrange("p (n t) -> p n t", t=4),
+                in1=r_sb[:].unsqueeze(1).to_broadcast([P, CHUNK, 4]),
+                op=MULT,
+            )
+
+        def kr_quantize(c):
+            quantize(krq[0][:, chunk_cols(c)], krq[1][:, chunk_cols(c)], kr_values[c][:])
+
+        def z_interleave(h):
+            split = Z_VECTOR_COLS[h]
+            dst = z_grouped[h][:].rearrange("p (c i) t -> p c t i", i=4)
+            src = z_raw[h][:].rearrange("p t (c i) -> p c t i", i=4)
+            if split > 0:
+                nc.vector.tensor_copy(out=dst[:, : split // 4], in_=src[:, : split // 4])
+            if split < HALF:
+                nc.scalar.copy(out=dst[:, split // 4 :], in_=src[:, split // 4 :])
+
+        def z_quantize(h):
+            cols = slice(h * HALF, (h + 1) * HALF)
+            quantize(zq[0][:, cols], zq[1][:, cols], z_grouped[h][:].rearrange("p c t -> p (c t)"))
+
+        def place(step):
+            c, h, e = step // 4, (step // 2) % 2, step % 2
+            return c, h, e
+
+        def kz_matmul(step):
+            c, h, e = place(step)
+            acc = bank(step % 2)
+            mx(acc[:], kq, tile_cols(2 * c + e), zq, slice(h * HALF, (h + 1) * HALF), True, True)
+            live["kz", step] = acc
+
+        def s_part(step):
+            c, h, e = place(step)
+            return s_raw[c][:, e, h * HALF : (h + 1) * HALF].rearrange("n (p t) -> n t p", t=4)
+
+        def widen_s(step):
+            wide = rotating("s_wide", [P, 4, P], F32, 3)
+            if CAST_ON_GPSIMD:
+                nc.gpsimd.tensor_scalar(out=wide[:], in0=s_part(step), scalar1=1.0, scalar2=0.0, op0=MULT, op1=ADD)
+            else:
+                nc.scalar.copy(out=wide[:], in_=s_part(step))
+            live["s", step] = wide
+
+        def subtract(step):
+            diff = rotating("diff", [P, 4, P], F32, 3)
+            kz = live["kz", step][:].rearrange("n (p t) -> n t p", t=4)
+            if step in PE_SUM_STEPS:
+                nc.scalar.activation(out=diff[:], in_=kz, func=COPY, scale=-1.0)
+            else:
+                nc.vector.tensor_tensor(out=diff[:], in0=s_part(step), in1=kz, op=SUB)
+            live["diff", step] = diff
+
+        def diff_transpose(step):
+            acc = bank(2 + step % 3)
+            for t in range(4):
+                if step in PE_SUM_STEPS:
+                    nc.tensor.matmul(acc[:, tile_cols(t)], lhsT=live["s", step][:, t, :], rhs=ident[:], is_transpose=True, start=True, stop=False)
+                    nc.tensor.matmul(acc[:, tile_cols(t)], lhsT=live["diff", step][:, t, :], rhs=ident[:], is_transpose=True, start=False, stop=True)
+                else:
+                    nc.tensor.transpose(acc[:, tile_cols(t)], live["diff", step][:, t, :], ident[:])
+            live["diffT", step] = acc
+
+        def scale(step):
+            c, h, e = place(step)
+            if e == 0:
+                live["w", c, h] = rotating("w_values", [P, 2, 2, P, 4], BF16, 2)
+            src = live["diffT", step][:].rearrange("p (t n) -> p n t", t=4)
+            nc.vector.tensor_tensor(
+                out=live["w", c, h][:, :, e],
+                in0=src.unsqueeze(1).to_broadcast([P, 2, P, 4]),
+                in1=factors[:, h].unsqueeze(2).to_broadcast([P, 2, P, 4]),
+                op=MULT,
+            )
+
+        def w_quantize(step):
+            c, h, e = place(step)
+            for j, dst in enumerate((wq[h], wdq[h])):
+                quantize(dst[0][:, chunk_cols(c)], dst[1][:, chunk_cols(c)], live["w", c, h][:, j].rearrange("p e n t -> p (e n t)"))
+
+        def result_passes(acc, i, cols):
+            mx(acc, krq, tile_cols(i), kq, cols, True, False)
+            mx(acc, wdq[0], tile_cols(i), wq[0], cols, False, False)
+            mx(acc, wdq[1], tile_cols(i), wq[1], cols, False, True)
+
+        def rounded(c, h):
+            if ("rounded", c, h) not in live:
+                live["rounded", c, h] = kept("rounded%d%d" % (c, h), [P, 2, 2, P, 2], BF16)
+            return live["rounded", c, h]
+
+        def unit_matmuls(unit, number):
+            acc = bank(number)
+            if unit[0] == "row":
+                result_passes(acc[:], unit[1], slice(unit[2] * HALF, (unit[2] + 1) * HALF))
+            else:
+                for e in range(2):
+                    result_passes(acc[:, chunk_cols(e)], 2 * unit[1] + e, chunk_cols(unit[2]))
+            live[unit] = acc
+
+        def copy_on(engine, out, in_):
+            if engine == "v":
+                nc.vector.tensor_copy(out=out, in_=in_)
+            else:
+                nc.scalar.copy(out=out, in_=in_)
+
+        def unit_out(unit, engine):
+            result = rotating("result", [P, HALF], F32, 6)
+            copy_on(engine, result[:], live[unit][:])
+            if unit[0] == "row":
+                i, h = unit[1], unit[2]
+                nc.sync.dma_start(out=out_0[tile_cols(i), h * HALF : (h + 1) * HALF], in_=result[:])
+            else:
+                c, q = unit[1], unit[2]
+                nc.sync.dma_start(
+                    out=out_0[chunk_cols(c), chunk_cols(q)].rearrange("(e n) m -> n e m", e=2),
+                    in_=result[:].rearrange("n (e m) -> n e m", e=2),
+                )
+            live["result", unit] = result
+
+        def unit_round(unit, engine):
+            result = live["result", unit]
+            if unit[0] == "row":
+                i, h = unit[1], unit[2]
+                copy_on(engine, rounded(i // 2, h)[:, i % 2], result[:].rearrange("n (p u v) -> n u p v", u=2, v=2))
+            else:
+                c, q = unit[1], unit[2]
+                part = slice((q % 2) * 64, (q % 2) * 64 + 64)
+                copy_on(engine, rounded(c, q // 2)[:, :, :, part, :], result[:].rearrange("n (e p u v) -> n e u p v", e=2, u=2, v=2))
+
+        def plane_transpose(c, h, number):
+            acc = bank(number)
+            words = rounded(c, h)[:].rearrange("n e u p v -> n (e u p v)").bitcast(F32)
+            for j in range(4):
+                nc.tensor.transpose(acc[:, tile_cols(j)], words[:, tile_cols(j)], ident[:])
+            live["planeT", c, h] = acc
+
+        def plane_words(c, h, engine):
+            grouped = rotating("plane_values", [P, HALF], F32, 3)
+            copy_on(
+                engine,
+                grouped[:].rearrange("p (e n u) -> p e n u", e=2, u=2),
+                live["planeT", c, h][:].rearrange("p (e u n) -> p e n u", e=2, u=2),
+            )
+            live["plane", c, h] = grouped
+
+        def plane_quantize(c, h):
+            codes = rotating("plane_codes", [P, CHUNK], U32, 4)
+            quantize(codes[:], plane_scales[h][:, chunk_cols(c)], live["plane", c, h][:].bitcast(BF16))
+            nc.sync.dma_start(out=words_out[h, :, chunk_cols(c)], in_=codes[:].bitcast(I32))
+
+        def plane_scale_stores(h):
+            for quad in range(4):
+                queue = nc.sync if quad % 2 == 0 else nc.scalar
+                queue.dma_start(
+                    out=scales_out[h, 4 * quad : 4 * quad + 4, :],
+                    in_=plane_scales[h][32 * quad : 32 * quad + 4, :].bitcast(I32),
+                )
+
+        k_transpose(0, 7)
+        z_interleave(0)
+        k_quantize(0)
+        z_quantize(0)
+        kz_matmul(0)
+        kz_matmul(1)
+        nc.vector.tensor_copy(out=factors[:, :, 0, :], in_=g_sb[:])
+        nc.vector.tensor_tensor(out=factors[:, :, 1, :], in0=g_sb[:], in1=d_sb[:], op=MULT)
+        kr_multiply(0)
+        for step in (0, 1):
+            if step in PE_SUM_STEPS:
+                widen_s(step)
+        subtract(0)
+        z_interleave(1)
+        diff_transpose(0)
+        kr_quantize(0)
+
+        early_units = {8: ("row", 0, 0), 9: ("row", 1, 0), 10: ("row", 2, 0), 11: ("row", 3, 0),
+                       12: ("row", 4, 0), 13: ("row", 5, 0), 14: ("pair", 0, 2), 15: ("pair", 1, 2)}
+        early_planes = {10: 0, 12: 1, 14: 2}
+        k_prepare = {1: 1, 4: 2, 6: 3}
+
+        for it in range(STEPS):
+            if it + 2 in PE_SUM_STEPS:
+                widen_s(it + 2)
+            if it + 1 < STEPS:
+                subtract(it + 1)
+            if it >= 2 and it % 2 == 0:
+                w_quantize(it - 1)
+            if it - 1 in k_prepare:
+                k_quantize(k_prepare[it - 1])
+            if it - 2 in k_prepare:
+                kr_quantize(k_prepare[it - 2])
+            if it - 1 in early_planes:
+                plane_quantize(early_planes[it - 1], 0)
+            if 0 < it and it + 2 < STEPS:
+                kz_matmul(it + 2)
+            if it in early_units:
+                unit_matmuls(early_units[it], 5 + it % 2)
+            if it + 1 < STEPS:
+                diff_transpose(it + 1)
+            if it in k_prepare:
+                k_transpose(k_prepare[it], 7)
+            if it in early_planes:
+                plane_transpose(early_planes[it], 0, 7)
+            if it in early_units:
+                unit_out(early_units[it], "s")
+                unit_round(early_units[it], "s")
+            if it in early_planes:
+                plane_words(early_planes[it], 0, "s")
+            scale(it)
+            if it - 1 in k_prepare:
+                kr_multiply(k_prepare[it - 1])
+            if it == 0:
+                z_quantize(1)
+                kz_matmul(2)
+
+        late = [("pair", 2, 2), ("pair", 0, 3), ("pair", 1, 3), ("pair", 2, 3),
+                ("row", 6, 0), ("row", 7, 0), ("row", 6, 1), ("row", 7, 1)]
+        unit_matmuls(late[0], 0)
+        unit_out(late[0], "s")
+        w_quantize(STEPS - 1)
+        unit_round(late[0], "s")
+        unit_matmuls(late[1], 1)
+        unit_matmuls(late[2], 5)
+        unit_out(late[1], "s")
+        unit_round(late[1], "v")
+        unit_matmuls(late[3], 6)
+        unit_out(late[2], "s")
+        unit_round(late[2], "v")
+        plane_transpose(0, 1, 2)
+        unit_matmuls(late[4], 0)
+        unit_out(late[3], "v")
+        plane_words(0, 1, "s")
+        unit_round(late[3], "v")
+        unit_matmuls(late[5], 1)
+        unit_out(late[4], "s")
+        plane_quantize(0, 1)
+        unit_round(late[4], "v")
+        plane_transpose(1, 1, 3)
+        plane_transpose(2, 1, 4)
+        unit_matmuls(late[6], 5)
+        unit_out(late[5], "s")
+        plane_words(1, 1, "v")
+        unit_round(late[5], "v")
+        unit_matmuls(late[7], 6)
+        plane_words(2, 1, "s")
+        plane_quantize(1, 1)
+        unit_out(late[6], "v")
+        plane_transpose(3, 0, 7)
+        unit_out(late[7], "s")
+        unit_round(late[6], "v")
+        plane_quantize(2, 1)
+        unit_round(late[7], "v")
+        plane_words(3, 0, "s")
+        plane_transpose(3, 1, 2)
+        plane_quantize(3, 0)
+        plane_words(3, 1, "s")
+        plane_scale_stores(0)
+        plane_quantize(3, 1)
+        plane_scale_stores(1)

@@ -22,8 +22,8 @@ HALF = 512
 CHUNK = 256
 STEPS = 16
 Z_VECTOR_COLS = (352, 0)
-PE_SUM_STEPS = ()
-CAST_ON_GPSIMD = False
+ROUTE = "VVGGGGGGGGGGGGGG"
+STEP_ORDER = [(i, h) for h in range(2) for i in range(4)] + [(i, h) for i in range(4, 8) for h in range(2)]
 
 
 def tile_josephkalmanupdate_x1_kernel(tc, s, z, kgain, g, d, r, out_0, out_1, out_2):
@@ -67,28 +67,31 @@ def tile_josephkalmanupdate_x1_kernel(tc, s, z, kgain, g, d, r, out_0, out_1, ou
         d_sb = kept("d_sb", [P, 2, 4], BF16)
         r_sb = kept("r_sb", [P, 4], BF16)
         k_raw = [kept("k_raw%d" % c, [P, 2, M], BF16) for c in range(4)]
-        s_raw = [kept("s_raw%d" % c, [P, 2, L], BF16) for c in range(4)]
+        s_raw = [[kept("s_raw%d%d" % (a, h), [P, 4, HALF], BF16) for h in range(2)] for a in range(2)]
         z_raw = [kept("z_raw%d" % h, [P, 4, HALF], BF16) for h in range(2)]
 
         def load_k(c):
             nc.sync.dma_start(out=k_raw[c][:], in_=kgain[c * CHUNK : (c + 1) * CHUNK, :].rearrange("(e p) m -> p e m", p=P))
 
-        def load_s(c):
-            nc.sync.dma_start(out=s_raw[c][:], in_=s[c * CHUNK : (c + 1) * CHUNK, :].rearrange("(e p) l -> p e l", p=P))
+        def load_s(a, h):
+            nc.sync.dma_start(out=s_raw[a][h][:], in_=s[a * HALF : (a + 1) * HALF, h * HALF : (h + 1) * HALF].rearrange("(e p) l -> p e l", p=P))
 
         def load_z(h):
             nc.sync.dma_start(out=z_raw[h][:], in_=z[:, h * HALF : (h + 1) * HALF].rearrange("(p j) l -> p j l", j=4))
 
         load_k(0)
         load_z(0)
-        nc.scalar.dma_start(out=r_sb[:], in_=r.rearrange("(p t) -> p t", t=4))
         nc.scalar.dma_start(out=g_sb[:], in_=g.rearrange("(h p t) -> p h t", h=2, t=4))
         nc.scalar.dma_start(out=d_sb[:], in_=d.rearrange("(h p t) -> p h t", h=2, t=4))
-        load_s(0)
+        nc.scalar.dma_start(out=r_sb[:], in_=r.rearrange("(p t) -> p t", t=4))
+        load_k(1)
+        load_s(0, 0)
         load_z(1)
-        for c in range(1, 4):
-            load_k(c)
-            load_s(c)
+        load_s(0, 1)
+        load_k(2)
+        load_k(3)
+        load_s(1, 0)
+        load_s(1, 1)
 
         ident = kept("ident", [P, P], F32)
         make_identity(nc, ident[:])
@@ -97,7 +100,7 @@ def tile_josephkalmanupdate_x1_kernel(tc, s, z, kgain, g, d, r, out_0, out_1, ou
         wq = [operand("wq%d" % h) for h in range(2)]
         wdq = [operand("wdq%d" % h) for h in range(2)]
         factors = kept("factors", [P, 2, 2, 4], F32)
-        plane_scales = [kept("plane_scales%d" % h, [P, N], U8) for h in range(2)]
+        plane_scales = kept("plane_scales", [P, N], U8)
         k_words = [kept("k_words%d" % c, [P, HALF], F32) for c in range(4)]
         kr_values = [kept("kr_values%d" % c, [P, 4 * CHUNK], BF16) for c in range(4)]
         z_grouped = [kept("z_grouped%d" % h, [P, HALF, 4], BF16) for h in range(2)]
@@ -134,95 +137,107 @@ def tile_josephkalmanupdate_x1_kernel(tc, s, z, kgain, g, d, r, out_0, out_1, ou
         def kr_quantize(c):
             quantize(krq[0][:, chunk_cols(c)], krq[1][:, chunk_cols(c)], kr_values[c][:])
 
-        def z_interleave(h):
-            split = Z_VECTOR_COLS[h]
-            dst = z_grouped[h][:].rearrange("p (c i) t -> p c t i", i=4)
-            src = z_raw[h][:].rearrange("p t (c i) -> p c t i", i=4)
-            if split > 0:
-                nc.vector.tensor_copy(out=dst[:, : split // 4], in_=src[:, : split // 4])
-            if split < HALF:
-                nc.scalar.copy(out=dst[:, split // 4 :], in_=src[:, split // 4 :])
+        def z_interleave(h, c0, c1, engine):
+            dst = z_grouped[h][:].rearrange("p (c i) t -> p c t i", i=4)[:, c0 // 4 : c1 // 4]
+            src = z_raw[h][:].rearrange("p t (c i) -> p c t i", i=4)[:, c0 // 4 : c1 // 4]
+            if engine == "g":
+                nc.gpsimd.tensor_scalar(out=dst, in0=src, scalar1=1.0, scalar2=0.0, op0=MULT, op1=ADD)
+            else:
+                copy_on(engine, dst, src)
 
         def z_quantize(h):
             cols = slice(h * HALF, (h + 1) * HALF)
             quantize(zq[0][:, cols], zq[1][:, cols], z_grouped[h][:].rearrange("p c t -> p (c t)"))
 
-        def place(step):
-            c, h, e = step // 4, (step // 2) % 2, step % 2
-            return c, h, e
+        def half_cols(h):
+            return slice(h * HALF, (h + 1) * HALF)
 
         def kz_matmul(step):
-            c, h, e = place(step)
-            acc = bank(step % 2)
-            mx(acc[:], kq, tile_cols(2 * c + e), zq, slice(h * HALF, (h + 1) * HALF), True, True)
-            live["kz", step] = acc
+            i, h = STEP_ORDER[step]
+            acc = bank((0, 1, 5, 6)[step % 4])
+            mx(acc[:], kq, tile_cols(i), zq, half_cols(h), True, True)
+            live["kz", step] = acc[:].rearrange("n (p t) -> n t p", t=4)
+
+        def kz_negate(step):
+            if ROUTE[step] != "V":
+                neg = kept("neg_kz%d" % step, [P, 4, P], F32)
+                nc.scalar.activation(out=neg[:], in_=live["kz", step], func=COPY, scale=-1.0)
+                live["neg", step] = neg
 
         def s_part(step):
-            c, h, e = place(step)
-            return s_raw[c][:, e, h * HALF : (h + 1) * HALF].rearrange("n (p t) -> n t p", t=4)
+            i, h = STEP_ORDER[step]
+            return s_raw[i // 4][h][:, i % 4, :].rearrange("n (p t) -> n t p", t=4)
 
         def widen_s(step):
-            wide = rotating("s_wide", [P, 4, P], F32, 3)
-            if CAST_ON_GPSIMD:
-                nc.gpsimd.tensor_scalar(out=wide[:], in0=s_part(step), scalar1=1.0, scalar2=0.0, op0=MULT, op1=ADD)
-            else:
-                nc.scalar.copy(out=wide[:], in_=s_part(step))
-            live["s", step] = wide
+            if ROUTE[step] in "PQ":
+                wide = rotating("s_wide", [P, 4, P], F32, 4)
+                if ROUTE[step] == "Q":
+                    nc.gpsimd.tensor_scalar(out=wide[:], in0=s_part(step), scalar1=1.0, scalar2=0.0, op0=MULT, op1=ADD)
+                else:
+                    nc.scalar.copy(out=wide[:], in_=s_part(step))
+                live["s", step] = wide
 
         def subtract(step):
-            diff = rotating("diff", [P, 4, P], F32, 3)
-            kz = live["kz", step][:].rearrange("n (p t) -> n t p", t=4)
-            if step in PE_SUM_STEPS:
-                nc.scalar.activation(out=diff[:], in_=kz, func=COPY, scale=-1.0)
+            if ROUTE[step] in "PQ":
+                return
+            diff = rotating("diff", [P, 4, P], F32, 4)
+            if ROUTE[step] == "V":
+                nc.vector.tensor_tensor(out=diff[:], in0=s_part(step), in1=live["kz", step], op=SUB)
+            elif ROUTE[step] == "S":
+                nc.vector.tensor_tensor(out=diff[:], in0=s_part(step), in1=live["neg", step][:], op=ADD)
             else:
-                nc.vector.tensor_tensor(out=diff[:], in0=s_part(step), in1=kz, op=SUB)
+                for t in (0, 2):
+                    nc.gpsimd.tensor_tensor(out=diff[:, t : t + 2], in0=s_part(step)[:, t : t + 2], in1=live["neg", step][:, t : t + 2], op=ADD)
             live["diff", step] = diff
 
         def diff_transpose(step):
             acc = bank(2 + step % 3)
             for t in range(4):
-                if step in PE_SUM_STEPS:
+                if ROUTE[step] in "PQ":
                     nc.tensor.matmul(acc[:, tile_cols(t)], lhsT=live["s", step][:, t, :], rhs=ident[:], is_transpose=True, start=True, stop=False)
-                    nc.tensor.matmul(acc[:, tile_cols(t)], lhsT=live["diff", step][:, t, :], rhs=ident[:], is_transpose=True, start=False, stop=True)
+                    nc.tensor.matmul(acc[:, tile_cols(t)], lhsT=live["neg", step][:, t, :], rhs=ident[:], is_transpose=True, start=False, stop=True)
                 else:
                     nc.tensor.transpose(acc[:, tile_cols(t)], live["diff", step][:, t, :], ident[:])
             live["diffT", step] = acc
 
         def scale(step):
-            c, h, e = place(step)
-            if e == 0:
-                live["w", c, h] = rotating("w_values", [P, 2, 2, P, 4], BF16, 2)
+            i, h = STEP_ORDER[step]
+            values = rotating("w_values", [P, 2, P, 4], BF16, 3)
             src = live["diffT", step][:].rearrange("p (t n) -> p n t", t=4)
             nc.vector.tensor_tensor(
-                out=live["w", c, h][:, :, e],
+                out=values[:],
                 in0=src.unsqueeze(1).to_broadcast([P, 2, P, 4]),
                 in1=factors[:, h].unsqueeze(2).to_broadcast([P, 2, P, 4]),
                 op=MULT,
             )
+            live["w", step] = values
 
         def w_quantize(step):
-            c, h, e = place(step)
+            i, h = STEP_ORDER[step]
             for j, dst in enumerate((wq[h], wdq[h])):
-                quantize(dst[0][:, chunk_cols(c)], dst[1][:, chunk_cols(c)], live["w", c, h][:, j].rearrange("p e n t -> p (e n t)"))
+                quantize(dst[0][:, tile_cols(i)], dst[1][:, tile_cols(i)], live["w", step][:, j].rearrange("p n t -> p (n t)"))
 
-        def result_passes(acc, i, cols):
-            mx(acc, krq, tile_cols(i), kq, cols, True, False)
-            mx(acc, wdq[0], tile_cols(i), wq[0], cols, False, False)
-            mx(acc, wdq[1], tile_cols(i), wq[1], cols, False, True)
+        operands = [(wdq[0], wq[0]), (wdq[1], wq[1]), (krq, kq)]
+
+        def unit_passes(unit, number, which=(0, 1, 2), rows=None):
+            first, count, col = unit
+            width = HALF // count
+            if unit not in live:
+                live[unit] = bank(number)
+                live["done", unit] = []
+            done = live["done", unit]
+            for k in which:
+                for e in range(count) if rows is None else rows:
+                    if (k, e) in done:
+                        continue
+                    done.append((k, e))
+                    mx(live[unit][:, e * width : (e + 1) * width], operands[k][0], tile_cols(first + e), operands[k][1],
+                       slice(col, col + width), len(done) == 1, len(done) == 3 * count)
 
         def rounded(c, h):
             if ("rounded", c, h) not in live:
                 live["rounded", c, h] = kept("rounded%d%d" % (c, h), [P, 2, 2, P, 2], BF16)
             return live["rounded", c, h]
-
-        def unit_matmuls(unit, number):
-            acc = bank(number)
-            if unit[0] == "row":
-                result_passes(acc[:], unit[1], slice(unit[2] * HALF, (unit[2] + 1) * HALF))
-            else:
-                for e in range(2):
-                    result_passes(acc[:, chunk_cols(e)], 2 * unit[1] + e, chunk_cols(unit[2]))
-            live[unit] = acc
 
         def copy_on(engine, out, in_):
             if engine == "v":
@@ -231,28 +246,25 @@ def tile_josephkalmanupdate_x1_kernel(tc, s, z, kgain, g, d, r, out_0, out_1, ou
                 nc.scalar.copy(out=out, in_=in_)
 
         def unit_out(unit, engine):
-            result = rotating("result", [P, HALF], F32, 6)
+            first, count, col = unit
+            width = HALF // count
+            result = rotating("result", [P, HALF], F32, 8)
             copy_on(engine, result[:], live[unit][:])
-            if unit[0] == "row":
-                i, h = unit[1], unit[2]
-                nc.sync.dma_start(out=out_0[tile_cols(i), h * HALF : (h + 1) * HALF], in_=result[:])
-            else:
-                c, q = unit[1], unit[2]
-                nc.sync.dma_start(
-                    out=out_0[chunk_cols(c), chunk_cols(q)].rearrange("(e n) m -> n e m", e=2),
-                    in_=result[:].rearrange("n (e m) -> n e m", e=2),
-                )
+            nc.sync.dma_start(
+                out=out_0[first * P : (first + count) * P, col : col + width].rearrange("(e n) m -> n e m", e=count),
+                in_=result[:].rearrange("n (e m) -> n e m", e=count),
+            )
             live["result", unit] = result
 
         def unit_round(unit, engine):
-            result = live["result", unit]
-            if unit[0] == "row":
-                i, h = unit[1], unit[2]
-                copy_on(engine, rounded(i // 2, h)[:, i % 2], result[:].rearrange("n (p u v) -> n u p v", u=2, v=2))
-            else:
-                c, q = unit[1], unit[2]
-                part = slice((q % 2) * 64, (q % 2) * 64 + 64)
-                copy_on(engine, rounded(c, q // 2)[:, :, :, part, :], result[:].rearrange("n (e p u v) -> n e u p v", e=2, u=2, v=2))
+            first, count, col = unit
+            width = HALF // count
+            h, p0 = col // HALF, (col % HALF) // 4
+            src = live["result", unit][:].rearrange("n (e p u v) -> n e u p v", e=count, u=2, v=2)
+            for e in range(0, count, 2):
+                rows = min(count, 2)
+                e0 = (first + e) % 2
+                copy_on(engine, rounded((first + e) // 2, h)[:, e0 : e0 + rows, :, p0 : p0 + width // 4, :], src[:, e : e + rows])
 
         def plane_transpose(c, h, number):
             acc = bank(number)
@@ -262,7 +274,7 @@ def tile_josephkalmanupdate_x1_kernel(tc, s, z, kgain, g, d, r, out_0, out_1, ou
             live["planeT", c, h] = acc
 
         def plane_words(c, h, engine):
-            grouped = rotating("plane_values", [P, HALF], F32, 3)
+            grouped = rotating("plane_values", [P, HALF], F32, 5)
             copy_on(
                 engine,
                 grouped[:].rearrange("p (e n u) -> p e n u", e=2, u=2),
@@ -271,116 +283,110 @@ def tile_josephkalmanupdate_x1_kernel(tc, s, z, kgain, g, d, r, out_0, out_1, ou
             live["plane", c, h] = grouped
 
         def plane_quantize(c, h):
-            codes = rotating("plane_codes", [P, CHUNK], U32, 4)
-            quantize(codes[:], plane_scales[h][:, chunk_cols(c)], live["plane", c, h][:].bitcast(BF16))
+            codes = rotating("plane_codes", [P, CHUNK], U32, 8)
+            quantize(codes[:], plane_scales[4 * h :, chunk_cols(c)], live["plane", c, h][:].bitcast(BF16))
             nc.sync.dma_start(out=words_out[h, :, chunk_cols(c)], in_=codes[:].bitcast(I32))
 
-        def plane_scale_stores(h):
+        def plane_scale_stores():
             for quad in range(4):
                 queue = nc.sync if quad % 2 == 0 else nc.scalar
                 queue.dma_start(
-                    out=scales_out[h, 4 * quad : 4 * quad + 4, :],
-                    in_=plane_scales[h][32 * quad : 32 * quad + 4, :].bitcast(I32),
+                    out=scales_out[:, 4 * quad : 4 * quad + 4, :],
+                    in_=plane_scales[32 * quad : 32 * quad + 8, :].bitcast(I32),
                 )
 
         k_transpose(0, 7)
-        z_interleave(0)
+        z_interleave(0, 0, 352, "v")
+        z_interleave(0, 352, 512, "s")
         k_quantize(0)
+        k_transpose(1, 2)
         z_quantize(0)
-        kz_matmul(0)
-        kz_matmul(1)
+        k_quantize(1)
+        for step in range(4):
+            kz_matmul(step)
         nc.vector.tensor_copy(out=factors[:, :, 0, :], in_=g_sb[:])
         nc.vector.tensor_tensor(out=factors[:, :, 1, :], in0=g_sb[:], in1=d_sb[:], op=MULT)
-        kr_multiply(0)
-        for step in (0, 1):
-            if step in PE_SUM_STEPS:
-                widen_s(step)
         subtract(0)
-        z_interleave(1)
+        subtract(1)
         diff_transpose(0)
-        kr_quantize(0)
+        diff_transpose(1)
+        z_interleave(1, 0, 256, "s")
+        kz_negate(2)
+        subtract(2)
+        kz_negate(3)
+        z_interleave(1, 256, 512, "s")
 
-        early_units = {8: ("row", 0, 0), 9: ("row", 1, 0), 10: ("row", 2, 0), 11: ("row", 3, 0),
-                       12: ("row", 4, 0), 13: ("row", 5, 0), 14: ("pair", 0, 2), 15: ("pair", 1, 2)}
-        early_planes = {10: 0, 12: 1, 14: 2}
-        k_prepare = {1: 1, 4: 2, 6: 3}
+        k_plan = {0: 2, 3: 3}
+        kq_plan = {2: 2, 5: 3}
+        kr_plan = {5: 0, 8: 1, 10: 2, 12: 3}
+        kz_plan = {1: [4, 5], 2: [6, 7], 3: [8, 9], 4: [10, 11], 5: [12, 13], 6: [14, 15]}
+        units = {7: [((0, 2, 0), 0)], 8: [((0, 2, 256), 1)], 9: [((2, 1, 0), 5), ((3, 1, 0), 6)], 10: [((0, 4, 512), 0)], 11: [((4, 1, 0), 1)], 12: [((5, 1, 0), 5), ((0, 4, 640), 6)], 13: [((4, 2, 512), 0)], 14: [((6, 1, 0), 1), ((0, 4, 768), 5)]}
+        planes = {10: 0, 11: 1, 14: 2}
 
-        for it in range(STEPS):
-            if it + 2 in PE_SUM_STEPS:
-                widen_s(it + 2)
-            if it + 1 < STEPS:
-                subtract(it + 1)
-            if it >= 2 and it % 2 == 0:
-                w_quantize(it - 1)
-            if it - 1 in k_prepare:
-                k_quantize(k_prepare[it - 1])
-            if it - 2 in k_prepare:
-                kr_quantize(k_prepare[it - 2])
-            if it - 1 in early_planes:
-                plane_quantize(early_planes[it - 1], 0)
-            if 0 < it and it + 2 < STEPS:
-                kz_matmul(it + 2)
-            if it in early_units:
-                unit_matmuls(early_units[it], 5 + it % 2)
-            if it + 1 < STEPS:
-                diff_transpose(it + 1)
-            if it in k_prepare:
-                k_transpose(k_prepare[it], 7)
-            if it in early_planes:
-                plane_transpose(early_planes[it], 0, 7)
-            if it in early_units:
-                unit_out(early_units[it], "s")
-                unit_round(early_units[it], "s")
-            if it in early_planes:
-                plane_words(early_planes[it], 0, "s")
-            scale(it)
-            if it - 1 in k_prepare:
-                kr_multiply(k_prepare[it - 1])
-            if it == 0:
+        for it in range(STEPS + 1):
+            if it < STEPS:
+                scale(it)
+            if it == 1:
                 z_quantize(1)
-                kz_matmul(2)
+            if it in kq_plan:
+                k_quantize(kq_plan[it])
+            if it >= 1:
+                w_quantize(it - 1)
+            if it - 1 in kr_plan:
+                kr_quantize(kr_plan[it - 1])
+            if it - 2 in planes:
+                plane_quantize(planes[it - 2], 0)
+            if it in kr_plan:
+                kr_multiply(kr_plan[it])
+            if it - 1 in planes:
+                plane_words(planes[it - 1], 0, "s")
+            for unit, number in units.get(it - 1, []):
+                unit_out(unit, "s")
+            for unit, number in units.get(it - 1, []):
+                unit_round(unit, "s")
+            if it + 2 < STEPS:
+                diff_transpose(it + 2)
+            if it in k_plan:
+                k_transpose(k_plan[it], 7)
+            if it in planes:
+                plane_transpose(planes[it], 0, 7)
+            for step in kz_plan.get(it, []):
+                kz_matmul(step)
+                kz_negate(step)
+            if it + 3 < STEPS:
+                subtract(it + 3)
+            for unit, number in units.get(it, []):
+                unit_passes(unit, number)
 
-        late = [("pair", 2, 2), ("pair", 0, 3), ("pair", 1, 3), ("pair", 2, 3),
-                ("row", 6, 0), ("row", 7, 0), ("row", 6, 1), ("row", 7, 1)]
-        unit_matmuls(late[0], 0)
-        unit_out(late[0], "s")
-        w_quantize(STEPS - 1)
-        unit_round(late[0], "s")
-        unit_matmuls(late[1], 1)
-        unit_matmuls(late[2], 5)
-        unit_out(late[1], "s")
-        unit_round(late[1], "v")
-        unit_matmuls(late[3], 6)
-        unit_out(late[2], "s")
-        unit_round(late[2], "v")
-        plane_transpose(0, 1, 2)
-        unit_matmuls(late[4], 0)
-        unit_out(late[3], "v")
-        plane_words(0, 1, "s")
-        unit_round(late[3], "v")
-        unit_matmuls(late[5], 1)
-        unit_out(late[4], "s")
-        plane_quantize(0, 1)
-        unit_round(late[4], "v")
-        plane_transpose(1, 1, 3)
-        plane_transpose(2, 1, 4)
-        unit_matmuls(late[6], 5)
-        unit_out(late[5], "s")
-        plane_words(1, 1, "v")
-        unit_round(late[5], "v")
-        unit_matmuls(late[7], 6)
-        plane_words(2, 1, "s")
-        plane_quantize(1, 1)
-        unit_out(late[6], "v")
+        col7a, col7b, row7, pair3, col6b = (0, 4, 896), (4, 4, 896), (7, 1, 0), (6, 2, 512), (4, 4, 768)
+        unit_passes(col7a, 6)
+        unit_passes(row7, 0)
+        unit_out(col7a, "v")
+        unit_round(col7a, "v")
+        unit_passes(col6b, 1)
+        unit_out(row7, "s")
+        unit_passes(col7b, 2)
+        unit_out(col6b, "v")
+        unit_round(row7, "s")
+        plane_transpose(0, 1, 3)
+        plane_transpose(1, 1, 4)
         plane_transpose(3, 0, 7)
-        unit_out(late[7], "s")
-        unit_round(late[6], "v")
-        plane_quantize(2, 1)
-        unit_round(late[7], "v")
+        unit_round(col6b, "v")
+        unit_passes(pair3, 5)
+        unit_out(col7b, "s")
+        plane_words(0, 1, "v")
+        unit_round(col7b, "v")
+        plane_words(1, 1, "s")
+        plane_transpose(2, 1, 6)
+        plane_quantize(0, 1)
+        unit_out(pair3, "v")
         plane_words(3, 0, "s")
-        plane_transpose(3, 1, 2)
+        plane_quantize(1, 1)
+        unit_round(pair3, "v")
+        plane_transpose(3, 1, 0)
+        plane_words(2, 1, "s")
         plane_quantize(3, 0)
         plane_words(3, 1, "s")
-        plane_scale_stores(0)
+        plane_quantize(2, 1)
         plane_quantize(3, 1)
-        plane_scale_stores(1)
+        plane_scale_stores()

@@ -18,12 +18,36 @@ ADD = mybir.AluOpType.add
 COPY = mybir.ActivationFunctionType.Copy
 
 P = 128
-HALF = 512
-CHUNK = 256
-STEPS = 16
-Z_VECTOR_COLS = (352, 0)
-ROUTE = "VVGGGGGGGGGGGGGG"
-STEP_ORDER = [(i, h) for h in range(2) for i in range(4)] + [(i, h) for i in range(4, 8) for h in range(2)]
+PACK = 4
+HALF = P * PACK
+PAIR = 2 * P
+
+STEPS = [(i, h) for h in range(2) for i in range(4)] + [(i, h) for i in range(4, 8) for h in range(2)]
+ROUNDS = len(STEPS) // 2
+
+Z_FIRST_ON_VECTOR = slice(0, 384)
+Z_FIRST_ON_SCALAR = slice(384, 512)
+Z_SECOND_ON_SCALAR = slice(0, 256)
+Z_SECOND_ON_VECTOR = slice(256, 512)
+
+J_FIRST, J_SECOND, Q_PASS = 0, 1, 2
+ALL_PASSES = (J_FIRST, J_SECOND, Q_PASS)
+
+
+def subtract_on(step):
+    if step in (0, 1, 3):
+        return "vector"
+    return "gpsimd" if step % 2 == 0 else "tensor"
+
+
+def kz_bank(step):
+    return (0, 1, 5, 6)[step % 4]
+
+
+def diff_bank(step):
+    if step % 2 == 0:
+        return 2
+    return 3 if step % 4 == 1 or step == len(STEPS) - 1 else 4
 
 
 def tile_josephkalmanupdate_x1_kernel(tc, s, z, kgain, g, d, r, out_0, out_1, out_2):
@@ -33,7 +57,7 @@ def tile_josephkalmanupdate_x1_kernel(tc, s, z, kgain, g, d, r, out_0, out_1, ou
 
     with ExitStack() as ctx:
         keep = ctx.enter_context(tc.tile_pool(name="keep", bufs=1))
-        work = ctx.enter_context(tc.tile_pool(name="work", bufs=3))
+        work = ctx.enter_context(tc.tile_pool(name="work", bufs=1))
         psum = ctx.enter_context(tc.psum_pool(name="psum", bufs=1))
         ctx.enter_context(tc.manual_schedule())
 
@@ -46,10 +70,19 @@ def tile_josephkalmanupdate_x1_kernel(tc, s, z, kgain, g, d, r, out_0, out_1, ou
         def rotating(name, shape, dtype, bufs):
             return work.tile(shape, dtype, name=name, tag=name, bufs=bufs, align_bytes=64)
 
-        def quantize(codes, scales, values):
-            nc.vector.quantize_mx(out=codes.bitcast(FP8X4), scales=scales, in_=values)
+        def handed_over(parity, shape, dtype):
+            return rotating("handed_over%d" % (parity % 2), shape, dtype, 1)
 
-        def mx(acc, lhs, lhs_cols, rhs, rhs_cols, start, stop):
+        def mx_operand(name):
+            return (kept(name + "_codes", [P, N], U32), kept(name + "_scales", [P, N], U8))
+
+        def cols(start, width):
+            return slice(start, start + width)
+
+        def quantize(operand, where, values):
+            nc.vector.quantize_mx(out=operand[0][:, where].bitcast(FP8X4), scales=operand[1][:, where], in_=values)
+
+        def mx_pass(acc, lhs, lhs_cols, rhs, rhs_cols, start, stop):
             nc.tensor.matmul_mx(
                 out=acc,
                 lhsT=lhs[0][:, lhs_cols].bitcast(FP8X4),
@@ -60,30 +93,34 @@ def tile_josephkalmanupdate_x1_kernel(tc, s, z, kgain, g, d, r, out_0, out_1, ou
                 stop=stop,
             )
 
-        def operand(name):
-            return (kept(name + "_codes", [P, N], U32), kept(name + "_scales", [P, N], U8))
+        def copy_on(engine, out, in_):
+            if engine == "vector":
+                nc.vector.tensor_copy(out=out, in_=in_)
+            else:
+                nc.scalar.copy(out=out, in_=in_)
 
-        g_sb = kept("g_sb", [P, 2, 4], BF16)
-        d_sb = kept("d_sb", [P, 2, 4], BF16)
-        r_sb = kept("r_sb", [P, 4], BF16)
+        g_sb = kept("g_sb", [P, 2, PACK], BF16)
+        d_sb = kept("d_sb", [P, 2, PACK], BF16)
+        r_sb = kept("r_sb", [P, PACK], BF16)
         k_raw = [kept("k_raw%d" % c, [P, 2, M], BF16) for c in range(4)]
         s_raw = [[kept("s_raw%d%d" % (a, h), [P, 4, HALF], BF16) for h in range(2)] for a in range(2)]
-        z_raw = [kept("z_raw%d" % h, [P, 4, HALF], BF16) for h in range(2)]
+        z_raw = [kept("z_raw%d" % h, [P, PACK, HALF], BF16) for h in range(2)]
 
         def load_k(c):
-            nc.sync.dma_start(out=k_raw[c][:], in_=kgain[c * CHUNK : (c + 1) * CHUNK, :].rearrange("(e p) m -> p e m", p=P))
+            nc.sync.dma_start(out=k_raw[c][:], in_=kgain[cols(c * PAIR, PAIR), :].rearrange("(e p) m -> p e m", p=P))
 
         def load_s(a, h):
-            nc.sync.dma_start(out=s_raw[a][h][:], in_=s[a * HALF : (a + 1) * HALF, h * HALF : (h + 1) * HALF].rearrange("(e p) l -> p e l", p=P))
+            rows = s[cols(a * HALF, HALF), cols(h * HALF, HALF)]
+            nc.sync.dma_start(out=s_raw[a][h][:], in_=rows.rearrange("(e p) l -> p e l", p=P))
 
         def load_z(h):
-            nc.sync.dma_start(out=z_raw[h][:], in_=z[:, h * HALF : (h + 1) * HALF].rearrange("(p j) l -> p j l", j=4))
+            nc.sync.dma_start(out=z_raw[h][:], in_=z[:, cols(h * HALF, HALF)].rearrange("(p t) l -> p t l", t=PACK))
 
         load_k(0)
         load_z(0)
-        nc.scalar.dma_start(out=g_sb[:], in_=g.rearrange("(h p t) -> p h t", h=2, t=4))
-        nc.scalar.dma_start(out=d_sb[:], in_=d.rearrange("(h p t) -> p h t", h=2, t=4))
-        nc.scalar.dma_start(out=r_sb[:], in_=r.rearrange("(p t) -> p t", t=4))
+        nc.scalar.dma_start(out=g_sb[:], in_=g.rearrange("(h p t) -> p h t", h=2, t=PACK))
+        nc.scalar.dma_start(out=d_sb[:], in_=d.rearrange("(h p t) -> p h t", h=2, t=PACK))
+        nc.scalar.dma_start(out=r_sb[:], in_=r.rearrange("(p t) -> p t", t=PACK))
         load_k(1)
         load_s(0, 0)
         load_z(1)
@@ -96,297 +133,351 @@ def tile_josephkalmanupdate_x1_kernel(tc, s, z, kgain, g, d, r, out_0, out_1, ou
         ident = kept("ident", [P, P], F32)
         make_identity(nc, ident[:])
 
-        kq, krq, zq = operand("kq"), operand("krq"), operand("zq")
-        wq = [operand("wq%d" % h) for h in range(2)]
-        wdq = [operand("wdq%d" % h) for h in range(2)]
-        factors = kept("factors", [P, 2, 2, 4], F32)
-        plane_scales = kept("plane_scales", [P, N], U8)
+        kq, krq, zq = mx_operand("kq"), mx_operand("krq"), mx_operand("zq")
+        wq = [mx_operand("wq%d" % h) for h in range(2)]
+        wdq = [mx_operand("wdq%d" % h) for h in range(2)]
+        pass_operands = [(wdq[0], wq[0]), (wdq[1], wq[1]), (krq, kq)]
+        factors = kept("factors", [P, 2, 2, PACK], F32)
+        out_scales = kept("out_scales", [P, N], U8)
         k_words = [kept("k_words%d" % c, [P, HALF], F32) for c in range(4)]
-        kr_values = [kept("kr_values%d" % c, [P, 4 * CHUNK], BF16) for c in range(4)]
-        z_grouped = [kept("z_grouped%d" % h, [P, HALF, 4], BF16) for h in range(2)]
-        live = {}
-
-        def chunk_cols(c):
-            return slice(c * CHUNK, (c + 1) * CHUNK)
-
-        def tile_cols(i):
-            return slice(i * P, (i + 1) * P)
+        kr_values = [kept("kr_values%d" % c, [P, PACK * PAIR], BF16) for c in range(4)]
+        z_grouped = [kept("z_grouped0", [P, HALF, PACK], BF16), handed_over(0, [P, HALF, PACK], BF16)]
+        kz, neg_kz, s_wide, diff, diff_t, w_values = {}, {}, {}, {}, {}, {}
+        unit_acc, unit_done, unit_result = {}, {}, {}
+        rounded, out_t, out_values = {}, {}, {}
 
         def k_transpose(c, number):
             acc = bank(number)
             for e in range(2):
                 words = k_raw[c][:, e, :].bitcast(F32)
                 for u in range(2):
-                    nc.tensor.transpose(acc[:, tile_cols(2 * e + u)], words[:, u::2], ident[:])
+                    nc.tensor.transpose(acc[:, cols((2 * e + u) * P, P)], words[:, u::2], ident[:])
             nc.scalar.copy(
                 out=k_words[c][:].rearrange("p (e n u) -> p e n u", e=2, u=2),
                 in_=acc[:].rearrange("p (e u n) -> p e n u", e=2, u=2),
             )
 
         def k_quantize(c):
-            quantize(kq[0][:, chunk_cols(c)], kq[1][:, chunk_cols(c)], k_words[c][:].bitcast(BF16))
+            quantize(kq, cols(c * PAIR, PAIR), k_words[c][:].bitcast(BF16))
 
         def kr_multiply(c):
             nc.vector.tensor_tensor(
-                out=kr_values[c][:].rearrange("p (n t) -> p n t", t=4),
-                in0=k_words[c][:].bitcast(BF16).rearrange("p (n t) -> p n t", t=4),
-                in1=r_sb[:].unsqueeze(1).to_broadcast([P, CHUNK, 4]),
+                out=kr_values[c][:].rearrange("p (n t) -> p n t", t=PACK),
+                in0=k_words[c][:].bitcast(BF16).rearrange("p (n t) -> p n t", t=PACK),
+                in1=r_sb[:].unsqueeze(1).to_broadcast([P, PAIR, PACK]),
                 op=MULT,
             )
 
         def kr_quantize(c):
-            quantize(krq[0][:, chunk_cols(c)], krq[1][:, chunk_cols(c)], kr_values[c][:])
+            quantize(krq, cols(c * PAIR, PAIR), kr_values[c][:])
 
-        def z_interleave(h, c0, c1, engine):
-            dst = z_grouped[h][:].rearrange("p (c i) t -> p c t i", i=4)[:, c0 // 4 : c1 // 4]
-            src = z_raw[h][:].rearrange("p t (c i) -> p c t i", i=4)[:, c0 // 4 : c1 // 4]
-            if engine == "g":
-                nc.gpsimd.tensor_scalar(out=dst, in0=src, scalar1=1.0, scalar2=0.0, op0=MULT, op1=ADD)
-            else:
-                copy_on(engine, dst, src)
+        def z_interleave(h, columns, engine):
+            groups = slice(columns.start // 4, columns.stop // 4)
+            copy_on(
+                engine,
+                z_grouped[h][:].rearrange("p (c i) t -> p c t i", i=4)[:, groups],
+                z_raw[h][:].rearrange("p t (c i) -> p c t i", i=4)[:, groups],
+            )
 
         def z_quantize(h):
-            cols = slice(h * HALF, (h + 1) * HALF)
-            quantize(zq[0][:, cols], zq[1][:, cols], z_grouped[h][:].rearrange("p c t -> p (c t)"))
-
-        def half_cols(h):
-            return slice(h * HALF, (h + 1) * HALF)
+            quantize(zq, cols(h * HALF, HALF), z_grouped[h][:].rearrange("p c t -> p (c t)"))
 
         def kz_matmul(step):
-            i, h = STEP_ORDER[step]
-            acc = bank((0, 1, 5, 6)[step % 4])
-            mx(acc[:], kq, tile_cols(i), zq, half_cols(h), True, True)
-            live["kz", step] = acc[:].rearrange("n (p t) -> n t p", t=4)
+            i, h = STEPS[step]
+            acc = bank(kz_bank(step))
+            mx_pass(acc[:], kq, cols(i * P, P), zq, cols(h * HALF, HALF), True, True)
+            kz[step] = acc[:].rearrange("n (p t) -> n t p", t=PACK)
 
         def kz_negate(step):
-            if ROUTE[step] != "V":
-                neg = kept("neg_kz%d" % step, [P, 4, P], F32)
-                nc.scalar.activation(out=neg[:], in_=live["kz", step], func=COPY, scale=-1.0)
-                live["neg", step] = neg
+            neg_kz[step] = kept("neg_kz%d" % step, [P, PACK, P], F32)
+            nc.scalar.activation(out=neg_kz[step][:], in_=kz[step], func=COPY, scale=-1.0)
 
         def s_part(step):
-            i, h = STEP_ORDER[step]
-            return s_raw[i // 4][h][:, i % 4, :].rearrange("n (p t) -> n t p", t=4)
+            i, h = STEPS[step]
+            return s_raw[i // 4][h][:, i % 4, :].rearrange("n (p t) -> n t p", t=PACK)
 
         def widen_s(step):
-            if ROUTE[step] in "PQ":
-                wide = rotating("s_wide", [P, 4, P], F32, 4)
-                if ROUTE[step] == "Q":
-                    nc.gpsimd.tensor_scalar(out=wide[:], in0=s_part(step), scalar1=1.0, scalar2=0.0, op0=MULT, op1=ADD)
-                else:
-                    nc.scalar.copy(out=wide[:], in_=s_part(step))
-                live["s", step] = wide
+            s_wide[step] = kept("s_wide%d" % step, [P, PACK, P], F32)
+            nc.scalar.copy(out=s_wide[step][:], in_=s_part(step))
 
-        def subtract(step):
-            if ROUTE[step] in "PQ":
-                return
-            diff = rotating("diff", [P, 4, P], F32, 4)
-            if ROUTE[step] == "V":
-                nc.vector.tensor_tensor(out=diff[:], in0=s_part(step), in1=live["kz", step], op=SUB)
-            elif ROUTE[step] == "S":
-                nc.vector.tensor_tensor(out=diff[:], in0=s_part(step), in1=live["neg", step][:], op=ADD)
-            else:
-                for t in (0, 2):
-                    nc.gpsimd.tensor_tensor(out=diff[:, t : t + 2], in0=s_part(step)[:, t : t + 2], in1=live["neg", step][:, t : t + 2], op=ADD)
-            live["diff", step] = diff
+        def subtract_on_vector(step):
+            diff[step] = kept("diff%d" % step, [P, PACK, P], F32)
+            nc.vector.tensor_tensor(out=diff[step][:], in0=s_part(step), in1=kz[step], op=SUB)
+
+        def subtract_on_gpsimd(step):
+            diff[step] = handed_over(step // 2 - 1, [P, PACK, P], F32)
+            for t in (0, 2):
+                slots = cols(t, 2)
+                nc.gpsimd.tensor_tensor(out=diff[step][:, slots], in0=s_part(step)[:, slots], in1=neg_kz[step][:, slots], op=ADD)
 
         def diff_transpose(step):
-            acc = bank(2 + step % 3)
-            for t in range(4):
-                if ROUTE[step] in "PQ":
-                    nc.tensor.matmul(acc[:, tile_cols(t)], lhsT=live["s", step][:, t, :], rhs=ident[:], is_transpose=True, start=True, stop=False)
-                    nc.tensor.matmul(acc[:, tile_cols(t)], lhsT=live["neg", step][:, t, :], rhs=ident[:], is_transpose=True, start=False, stop=True)
+            acc = bank(diff_bank(step))
+            for t in range(PACK):
+                slot = acc[:, cols(t * P, P)]
+                if subtract_on(step) == "tensor":
+                    nc.tensor.matmul(slot, lhsT=s_wide[step][:, t, :], rhs=ident[:], is_transpose=True, start=True, stop=False)
+                    nc.tensor.matmul(slot, lhsT=neg_kz[step][:, t, :], rhs=ident[:], is_transpose=True, start=False, stop=True)
                 else:
-                    nc.tensor.transpose(acc[:, tile_cols(t)], live["diff", step][:, t, :], ident[:])
-            live["diffT", step] = acc
+                    nc.tensor.transpose(slot, diff[step][:, t, :], ident[:])
+            diff_t[step] = acc
 
         def scale(step):
-            i, h = STEP_ORDER[step]
-            values = rotating("w_values", [P, 2, P, 4], BF16, 3)
-            src = live["diffT", step][:].rearrange("p (t n) -> p n t", t=4)
+            h = STEPS[step][1]
+            shape = [P, 2, P, PACK]
+            if step % 2 == 1:
+                w_values[step] = handed_over(step // 2 + 1, shape, BF16)
+            else:
+                w_values[step] = rotating("w_values", shape, BF16, 2)
             nc.vector.tensor_tensor(
-                out=values[:],
-                in0=src.unsqueeze(1).to_broadcast([P, 2, P, 4]),
-                in1=factors[:, h].unsqueeze(2).to_broadcast([P, 2, P, 4]),
+                out=w_values[step][:],
+                in0=diff_t[step][:].rearrange("p (t n) -> p n t", t=PACK).unsqueeze(1).to_broadcast(shape),
+                in1=factors[:, h].unsqueeze(2).to_broadcast(shape),
                 op=MULT,
             )
-            live["w", step] = values
 
         def w_quantize(step):
-            i, h = STEP_ORDER[step]
-            for j, dst in enumerate((wq[h], wdq[h])):
-                quantize(dst[0][:, tile_cols(i)], dst[1][:, tile_cols(i)], live["w", step][:, j].rearrange("p n t -> p (n t)"))
+            i, h = STEPS[step]
+            quantize(wq[h], cols(i * P, P), w_values[step][:, 0].rearrange("p n t -> p (n t)"))
 
-        operands = [(wdq[0], wq[0]), (wdq[1], wq[1]), (krq, kq)]
+        def wd_quantize(step):
+            i, h = STEPS[step]
+            quantize(wdq[h], cols(i * P, P), w_values[step][:, 1].rearrange("p n t -> p (n t)"))
 
-        def unit_passes(unit, number, which=(0, 1, 2), rows=None):
+        def unit_open(unit, number):
+            unit_acc[unit] = bank(number)
+            unit_done[unit] = 0
+
+        def unit_passes(unit, passes):
             first, count, col = unit
             width = HALF // count
-            if unit not in live:
-                live[unit] = bank(number)
-                live["done", unit] = []
-            done = live["done", unit]
-            for k in which:
-                for e in range(count) if rows is None else rows:
-                    if (k, e) in done:
-                        continue
-                    done.append((k, e))
-                    mx(live[unit][:, e * width : (e + 1) * width], operands[k][0], tile_cols(first + e), operands[k][1],
-                       slice(col, col + width), len(done) == 1, len(done) == 3 * count)
+            for k in passes:
+                lhs, rhs = pass_operands[k]
+                for e in range(count):
+                    unit_done[unit] = unit_done[unit] + 1
+                    mx_pass(
+                        unit_acc[unit][:, cols(e * width, width)], lhs, cols((first + e) * P, P), rhs, cols(col, width),
+                        unit_done[unit] == 1, unit_done[unit] == len(ALL_PASSES) * count,
+                    )
 
-        def rounded(c, h):
-            if ("rounded", c, h) not in live:
-                live["rounded", c, h] = kept("rounded%d%d" % (c, h), [P, 2, 2, P, 2], BF16)
-            return live["rounded", c, h]
-
-        def copy_on(engine, out, in_):
-            if engine == "v":
-                nc.vector.tensor_copy(out=out, in_=in_)
-            else:
-                nc.scalar.copy(out=out, in_=in_)
-
-        def unit_out(unit, engine):
+        def unit_store(unit, engine):
             first, count, col = unit
-            width = HALF // count
-            result = rotating("result", [P, HALF], F32, 8)
-            copy_on(engine, result[:], live[unit][:])
+            unit_result[unit] = rotating("result", [P, HALF], F32, 10)
+            copy_on(engine, unit_result[unit][:], unit_acc[unit][:])
             nc.sync.dma_start(
-                out=out_0[first * P : (first + count) * P, col : col + width].rearrange("(e n) m -> n e m", e=count),
-                in_=result[:].rearrange("n (e m) -> n e m", e=count),
+                out=out_0[cols(first * P, count * P), cols(col, HALF // count)].rearrange("(e n) m -> n e m", e=count),
+                in_=unit_result[unit][:].rearrange("n (e m) -> n e m", e=count),
             )
-            live["result", unit] = result
 
         def unit_round(unit, engine):
             first, count, col = unit
-            width = HALF // count
-            h, p0 = col // HALF, (col % HALF) // 4
-            src = live["result", unit][:].rearrange("n (e p u v) -> n e u p v", e=count, u=2, v=2)
-            for e in range(0, count, 2):
-                rows = min(count, 2)
-                e0 = (first + e) % 2
-                copy_on(engine, rounded((first + e) // 2, h)[:, e0 : e0 + rows, :, p0 : p0 + width // 4, :], src[:, e : e + rows])
+            h, partitions = col // HALF, cols((col % HALF) // PACK, P // count)
+            src = unit_result[unit][:].rearrange("n (e p u v) -> n e u p v", e=count, u=2, v=2)
+            tiles = min(count, 2)
+            for e in range(0, count, tiles):
+                c = (first + e) // 2
+                if (c, h) not in rounded:
+                    rounded[c, h] = kept("rounded%d%d" % (c, h), [P, 2, 2, P, 2], BF16)
+                copy_on(engine, rounded[c, h][:, cols((first + e) % 2, tiles), :, partitions, :], src[:, cols(e, tiles)])
 
-        def plane_transpose(c, h, number):
-            acc = bank(number)
-            words = rounded(c, h)[:].rearrange("n e u p v -> n (e u p v)").bitcast(F32)
+        def out_transpose(c, h, number):
+            out_t[c, h] = bank(number)
+            words = rounded[c, h][:].rearrange("n e u p v -> n (e u p v)").bitcast(F32)
             for j in range(4):
-                nc.tensor.transpose(acc[:, tile_cols(j)], words[:, tile_cols(j)], ident[:])
-            live["planeT", c, h] = acc
+                nc.tensor.transpose(out_t[c, h][:, cols(j * P, P)], words[:, cols(j * P, P)], ident[:])
 
-        def plane_words(c, h, engine):
-            grouped = rotating("plane_values", [P, HALF], F32, 5)
+        def out_interleave(c, h, engine):
+            out_values[c, h] = rotating("out_values", [P, HALF], F32, 5)
             copy_on(
                 engine,
-                grouped[:].rearrange("p (e n u) -> p e n u", e=2, u=2),
-                live["planeT", c, h][:].rearrange("p (e u n) -> p e n u", e=2, u=2),
+                out_values[c, h][:].rearrange("p (e n u) -> p e n u", e=2, u=2),
+                out_t[c, h][:].rearrange("p (e u n) -> p e n u", e=2, u=2),
             )
-            live["plane", c, h] = grouped
 
-        def plane_quantize(c, h):
-            codes = rotating("plane_codes", [P, CHUNK], U32, 8)
-            quantize(codes[:], plane_scales[4 * h :, chunk_cols(c)], live["plane", c, h][:].bitcast(BF16))
-            nc.sync.dma_start(out=words_out[h, :, chunk_cols(c)], in_=codes[:].bitcast(I32))
-
-        def plane_scale_stores():
-            for quad in range(4):
-                queue = nc.sync if quad % 2 == 0 else nc.scalar
-                queue.dma_start(
-                    out=scales_out[:, 4 * quad : 4 * quad + 4, :],
-                    in_=plane_scales[32 * quad : 32 * quad + 8, :].bitcast(I32),
-                )
+        def out_quantize(c, h):
+            codes = kept("out_codes%d%d" % (c, h), [P, PAIR], U32)
+            nc.vector.quantize_mx(
+                out=codes[:].bitcast(FP8X4),
+                scales=out_scales[4 * h :, cols(c * PAIR, PAIR)],
+                in_=out_values[c, h][:].bitcast(BF16),
+            )
+            nc.sync.dma_start(out=words_out[h, :, cols(c * PAIR, PAIR)], in_=codes[:].bitcast(I32))
 
         k_transpose(0, 7)
-        z_interleave(0, 0, 352, "v")
-        z_interleave(0, 352, 512, "s")
+        z_interleave(0, Z_FIRST_ON_VECTOR, "vector")
+        z_interleave(0, Z_FIRST_ON_SCALAR, "scalar")
         k_quantize(0)
         k_transpose(1, 2)
         z_quantize(0)
+        kz_matmul(0)
+        kz_matmul(1)
+        kr_multiply(0)
         k_quantize(1)
-        for step in range(4):
-            kz_matmul(step)
-        nc.vector.tensor_copy(out=factors[:, :, 0, :], in_=g_sb[:])
-        nc.vector.tensor_tensor(out=factors[:, :, 1, :], in0=g_sb[:], in1=d_sb[:], op=MULT)
-        subtract(0)
-        subtract(1)
+        kz_matmul(2)
+        kz_matmul(3)
+        z_interleave(1, Z_SECOND_ON_SCALAR, "scalar")
+        subtract_on_vector(0)
+        subtract_on_vector(1)
         diff_transpose(0)
         diff_transpose(1)
-        z_interleave(1, 0, 256, "s")
+        k_transpose(2, 7)
+        nc.vector.tensor_copy(out=factors[:, :, 0, :], in_=g_sb[:])
+        nc.vector.tensor_tensor(out=factors[:, :, 1, :], in0=g_sb[:], in1=d_sb[:], op=MULT)
+        z_interleave(1, Z_SECOND_ON_VECTOR, "vector")
+        z_quantize(1)
         kz_negate(2)
-        subtract(2)
-        kz_negate(3)
-        z_interleave(1, 256, 512, "s")
 
-        k_plan = {0: 2, 3: 3}
-        kq_plan = {2: 2, 5: 3}
-        kr_plan = {5: 0, 8: 1, 10: 2, 12: 3}
-        kz_plan = {1: [4, 5], 2: [6, 7], 3: [8, 9], 4: [10, 11], 5: [12, 13], 6: [14, 15]}
-        units = {7: [((0, 2, 0), 0)], 8: [((0, 2, 256), 1)], 9: [((2, 1, 0), 5), ((3, 1, 0), 6)], 10: [((0, 4, 512), 0)], 11: [((4, 1, 0), 1)], 12: [((5, 1, 0), 5), ((0, 4, 640), 6)], 13: [((4, 2, 512), 0)], 14: [((6, 1, 0), 1), ((0, 4, 768), 5)]}
-        planes = {10: 0, 11: 1, 14: 2}
+        def round_start(j):
+            subtract_on_gpsimd(2 * j + 2)
+            scale(2 * j)
+            if subtract_on(2 * j + 3) == "vector":
+                subtract_on_vector(2 * j + 3)
+            scale(2 * j + 1)
 
-        for it in range(STEPS + 1):
-            if it < STEPS:
-                scale(it)
-            if it == 1:
-                z_quantize(1)
-            if it in kq_plan:
-                k_quantize(kq_plan[it])
-            if it >= 1:
-                w_quantize(it - 1)
-            if it - 1 in kr_plan:
-                kr_quantize(kr_plan[it - 1])
-            if it - 2 in planes:
-                plane_quantize(planes[it - 2], 0)
-            if it in kr_plan:
-                kr_multiply(kr_plan[it])
-            if it - 1 in planes:
-                plane_words(planes[it - 1], 0, "s")
-            for unit, number in units.get(it - 1, []):
-                unit_out(unit, "s")
-            for unit, number in units.get(it - 1, []):
-                unit_round(unit, "s")
-            if it + 2 < STEPS:
-                diff_transpose(it + 2)
-            if it in k_plan:
-                k_transpose(k_plan[it], 7)
-            if it in planes:
-                plane_transpose(planes[it], 0, 7)
-            for step in kz_plan.get(it, []):
-                kz_matmul(step)
+        def round_quantize(j, kr_pair=None, k_pair=None, kr_ready=None, out_block=None, finished=()):
+            if kr_pair is not None:
+                kr_multiply(kr_pair)
+            wd_quantize(2 * j)
+            w_quantize(2 * j)
+            for unit in finished:
+                unit_round(unit, "scalar")
+            if k_pair is not None:
+                k_quantize(k_pair)
+            if out_block is not None:
+                out_quantize(*out_block)
+            if kr_ready is not None:
+                kr_quantize(kr_ready)
+            w_quantize(2 * j + 1)
+            wd_quantize(2 * j + 1)
+
+        for j in range(3):
+            ahead = range(4 * j + 4, 4 * j + 8)
+            round_start(j)
+            kz_matmul(ahead[0])
+            kz_matmul(ahead[1])
+            if j == 0:
+                k_transpose(3, 4)
+            else:
+                diff_transpose(2 * j + 3)
+            kz_matmul(ahead[2])
+            kz_matmul(ahead[3])
+            if j > 0:
+                widen_s(2 * j + 5)
+            for step in ahead:
                 kz_negate(step)
-            if it + 3 < STEPS:
-                subtract(it + 3)
-            for unit, number in units.get(it, []):
-                unit_passes(unit, number)
+                if step == 5:
+                    widen_s(step)
+            diff_transpose(2 * j + 2)
+            if j == 0:
+                diff_transpose(2 * j + 3)
+            round_quantize(j, k_pair=j + 2 if j < 2 else None, kr_ready=0 if j == 0 else None)
 
-        col7a, col7b, row7, pair3, col6b = (0, 4, 896), (4, 4, 896), (7, 1, 0), (6, 2, 512), (4, 4, 768)
-        unit_passes(col7a, 6)
-        unit_passes(row7, 0)
-        unit_out(col7a, "v")
-        unit_round(col7a, "v")
-        unit_passes(col6b, 1)
-        unit_out(row7, "s")
-        unit_passes(col7b, 2)
-        unit_out(col6b, "v")
-        unit_round(row7, "s")
-        plane_transpose(0, 1, 3)
-        plane_transpose(1, 1, 4)
-        plane_transpose(3, 0, 7)
-        unit_round(col6b, "v")
-        unit_passes(pair3, 5)
-        unit_out(col7b, "s")
-        plane_words(0, 1, "v")
-        unit_round(col7b, "v")
-        plane_words(1, 1, "s")
-        plane_transpose(2, 1, 6)
-        plane_quantize(0, 1)
-        unit_out(pair3, "v")
-        plane_words(3, 0, "s")
-        plane_quantize(1, 1)
-        unit_round(pair3, "v")
-        plane_transpose(3, 1, 0)
-        plane_words(2, 1, "s")
-        plane_quantize(3, 0)
-        plane_words(3, 1, "s")
-        plane_quantize(2, 1)
-        plane_quantize(3, 1)
-        plane_scale_stores()
+        top_left = [(i, 1, 0) for i in range(4)]
+        round_start(3)
+        for unit, number in zip(top_left[:2], (0, 1)):
+            unit_open(unit, number)
+            unit_passes(unit, (J_FIRST, Q_PASS))
+        diff_transpose(9)
+        for step in (11, 13, 15):
+            widen_s(step)
+        for unit, number in zip(top_left[2:], (5, 6)):
+            unit_open(unit, number)
+            unit_passes(unit, (J_FIRST,))
+        diff_transpose(8)
+        round_quantize(3, kr_pair=1, kr_ready=1)
+
+        def round_results(j, finish, block_before, block_now, open_next):
+            round_start(j)
+            for unit, number, passes in finish:
+                if number is not None:
+                    unit_open(unit, number)
+                unit_passes(unit, passes)
+            if block_before is not None:
+                out_interleave(*block_before, "scalar")
+            for unit, number, passes in finish:
+                unit_store(unit, "scalar")
+            diff_transpose(2 * j + 2)
+            diff_transpose(2 * j + 3)
+            if block_now is not None:
+                out_transpose(*block_now, 7)
+            for unit, number in open_next:
+                unit_open(unit, number)
+                unit_passes(unit, (Q_PASS,))
+
+        both_j = (J_FIRST, J_SECOND)
+        column4, column5, column6, column7 = [(0, 4, i * P) for i in range(4, 8)]
+        row4, row5, row6, row7 = [(i, 1, 0) for i in range(4, 8)]
+        corner_a, corner_b = (4, 2, 512), (4, 2, 768)
+        corner_c, corner_d = (6, 2, 512), (6, 2, 768)
+
+        finish = [(unit, None, (J_SECOND,)) for unit in top_left[:2]] + [(unit, None, (Q_PASS, J_SECOND)) for unit in top_left[2:]]
+        round_results(4, finish, None, None, [(column4, 1)])
+        round_quantize(4, kr_pair=2, kr_ready=2, finished=top_left)
+
+        finish = [(row4, 0, ALL_PASSES), (column4, None, both_j)]
+        round_results(5, finish, None, (0, 0), [(column5, 5), (corner_a, 6)])
+        round_quantize(5, finished=[row4, column4])
+
+        finish = [(row5, 4, ALL_PASSES), (column5, None, both_j), (corner_a, None, both_j)]
+        round_results(6, finish, (0, 0), (1, 0), [])
+        round_quantize(6, kr_pair=3, kr_ready=3, out_block=(0, 0), finished=[row5, column5, corner_a])
+
+        last = 2 * (ROUNDS - 1)
+        scale(last)
+        for unit, number in ((row6, 0), (column6, 1)):
+            unit_open(unit, number)
+            unit_passes(unit, ALL_PASSES)
+        out_interleave(1, 0, "scalar")
+        unit_store(row6, "scalar")
+        unit_store(column6, "scalar")
+        w_quantize(last)
+        wd_quantize(last)
+        scale(last + 1)
+        out_transpose(2, 0, 7)
+        for unit, number in ((column7, 4), (row7, 2)):
+            unit_open(unit, number)
+            unit_passes(unit, (Q_PASS, J_FIRST))
+        w_quantize(last + 1)
+        wd_quantize(last + 1)
+
+        unit_passes(column7, (J_SECOND,))
+        unit_passes(row7, (J_SECOND,))
+        unit_open(corner_b, 5)
+        unit_passes(corner_b, ALL_PASSES)
+        out_quantize(1, 0)
+        unit_round(column6, "vector")
+        out_interleave(2, 0, "scalar")
+        unit_round(row6, "vector")
+        unit_store(column7, "scalar")
+        unit_open(corner_c, 6)
+        unit_passes(corner_c, ALL_PASSES)
+        unit_store(row7, "vector")
+        unit_open(corner_d, 7)
+        unit_passes(corner_d, ALL_PASSES)
+        unit_round(column7, "vector")
+        unit_store(corner_b, "scalar")
+        unit_round(row7, "vector")
+        out_transpose(0, 1, 0)
+        out_transpose(1, 1, 1)
+        out_transpose(3, 0, 3)
+        unit_store(corner_c, "scalar")
+        unit_round(corner_b, "vector")
+        out_transpose(2, 1, 4)
+        unit_store(corner_d, "vector")
+        unit_round(corner_c, "vector")
+        out_interleave(0, 1, "scalar")
+        unit_round(corner_d, "vector")
+        out_transpose(3, 1, 2)
+        out_interleave(1, 1, "scalar")
+        out_quantize(2, 0)
+        out_interleave(3, 0, "vector")
+        out_interleave(2, 1, "scalar")
+        out_quantize(0, 1)
+        out_quantize(1, 1)
+        out_interleave(3, 1, "scalar")
+        out_quantize(3, 0)
+        out_quantize(2, 1)
+        out_quantize(3, 1)
+
+        for quad in range(4):
+            queue = nc.sync if quad % 2 == 0 else nc.scalar
+            queue.dma_start(out=scales_out[:, cols(4 * quad, 4), :], in_=out_scales[cols(32 * quad, 8), :].bitcast(I32))

@@ -23,21 +23,18 @@ HALF = P * PACK
 PAIR = 2 * P
 
 STEPS = [(i, h) for h in range(2) for i in range(4)] + [(i, h) for i in range(4, 8) for h in range(2)]
-ROUNDS = len(STEPS) // 2
 
 Z_FIRST_ON_VECTOR = slice(0, 384)
 Z_FIRST_ON_SCALAR = slice(384, 512)
-Z_SECOND_ON_SCALAR = slice(0, 256)
-Z_SECOND_ON_VECTOR = slice(256, 512)
+Z_SECOND_ON_SCALAR = slice(0, 320)
+Z_SECOND_ON_VECTOR = slice(320, 512)
 
 J_FIRST, J_SECOND, Q_PASS = 0, 1, 2
 ALL_PASSES = (J_FIRST, J_SECOND, Q_PASS)
 
 
-def subtract_on(step):
-    if step in (0, 1, 3):
-        return "vector"
-    return "gpsimd" if step % 2 == 0 else "tensor"
+def summed_in_psum(step):
+    return step > 1 and step % 2 == 1
 
 
 def kz_bank(step):
@@ -47,7 +44,7 @@ def kz_bank(step):
 def diff_bank(step):
     if step % 2 == 0:
         return 2
-    return 3 if step % 4 == 1 or step == len(STEPS) - 1 else 4
+    return 3 if step % 4 == 1 else 4
 
 
 def tile_josephkalmanupdate_x1_kernel(tc, s, z, kgain, g, d, r, out_0, out_1, out_2):
@@ -214,7 +211,7 @@ def tile_josephkalmanupdate_x1_kernel(tc, s, z, kgain, g, d, r, out_0, out_1, ou
             acc = bank(diff_bank(step))
             for t in range(PACK):
                 slot = acc[:, cols(t * P, P)]
-                if subtract_on(step) == "tensor":
+                if summed_in_psum(step):
                     nc.tensor.matmul(slot, lhsT=s_wide[step][:, t, :], rhs=ident[:], is_transpose=True, start=True, stop=False)
                     nc.tensor.matmul(slot, lhsT=neg_kz[step][:, t, :], rhs=ident[:], is_transpose=True, start=False, stop=True)
                 else:
@@ -319,156 +316,175 @@ def tile_josephkalmanupdate_x1_kernel(tc, s, z, kgain, g, d, r, out_0, out_1, ou
         subtract_on_vector(1)
         diff_transpose(0)
         diff_transpose(1)
+        widen_s(3)
+        kz_negate(2)
+        kz_negate(3)
         k_transpose(2, 7)
         nc.vector.tensor_copy(out=factors[:, :, 0, :], in_=g_sb[:])
         nc.vector.tensor_tensor(out=factors[:, :, 1, :], in0=g_sb[:], in1=d_sb[:], op=MULT)
         z_interleave(1, Z_SECOND_ON_VECTOR, "vector")
         z_quantize(1)
-        kz_negate(2)
 
-        def round_start(j):
+        def round_scale(j):
             subtract_on_gpsimd(2 * j + 2)
             scale(2 * j)
-            if subtract_on(2 * j + 3) == "vector":
-                subtract_on_vector(2 * j + 3)
             scale(2 * j + 1)
 
-        def round_quantize(j, kr_pair=None, k_pair=None, kr_ready=None, out_block=None, finished=()):
-            if kr_pair is not None:
-                kr_multiply(kr_pair)
+        def quantize_even(j):
             wd_quantize(2 * j)
             w_quantize(2 * j)
-            for unit in finished:
-                unit_round(unit, "scalar")
-            if k_pair is not None:
-                k_quantize(k_pair)
-            if out_block is not None:
-                out_quantize(*out_block)
-            if kr_ready is not None:
-                kr_quantize(kr_ready)
+
+        def quantize_odd(j):
             w_quantize(2 * j + 1)
             wd_quantize(2 * j + 1)
 
-        for j in range(3):
+        def open_with(units, numbers, passes):
+            for unit, number in zip(units, numbers):
+                unit_open(unit, number)
+                unit_passes(unit, passes)
+
+        def go_on_with(units, passes):
+            for unit in units:
+                unit_passes(unit, passes)
+
+        def store_on_scalar(units):
+            for unit in units:
+                unit_store(unit, "scalar")
+
+        def round_on_scalar(units):
+            for unit in units:
+                unit_round(unit, "scalar")
+
+        round_scale(0)
+        kz_matmul(4)
+        kz_matmul(5)
+        k_transpose(3, 4)
+        kz_matmul(6)
+        kz_matmul(7)
+        kz_negate(4)
+        kz_negate(5)
+        widen_s(5)
+        kz_negate(6)
+        kz_negate(7)
+        diff_transpose(2)
+        diff_transpose(3)
+        quantize_even(0)
+        k_quantize(2)
+        kr_quantize(0)
+        quantize_odd(0)
+
+        for j in (1, 2):
             ahead = range(4 * j + 4, 4 * j + 8)
-            round_start(j)
+            round_scale(j)
             kz_matmul(ahead[0])
             kz_matmul(ahead[1])
-            if j == 0:
-                k_transpose(3, 4)
-            else:
-                diff_transpose(2 * j + 3)
+            diff_transpose(2 * j + 3)
             kz_matmul(ahead[2])
             kz_matmul(ahead[3])
-            if j > 0:
-                widen_s(2 * j + 5)
+            widen_s(2 * j + 5)
             for step in ahead:
                 kz_negate(step)
-                if step == 5:
-                    widen_s(step)
             diff_transpose(2 * j + 2)
-            if j == 0:
-                diff_transpose(2 * j + 3)
-            round_quantize(j, k_pair=j + 2 if j < 2 else None, kr_ready=0 if j == 0 else None)
-
-        top_left = [(i, 1, 0) for i in range(4)]
-        round_start(3)
-        for unit, number in zip(top_left[:2], (0, 1)):
-            unit_open(unit, number)
-            unit_passes(unit, (J_FIRST, Q_PASS))
-        diff_transpose(9)
-        for step in (11, 13, 15):
-            widen_s(step)
-        for unit, number in zip(top_left[2:], (5, 6)):
-            unit_open(unit, number)
-            unit_passes(unit, (J_FIRST,))
-        diff_transpose(8)
-        round_quantize(3, kr_pair=1, kr_ready=1)
-
-        def round_results(j, finish, block_before, block_now, open_next):
-            round_start(j)
-            for unit, number, passes in finish:
-                if number is not None:
-                    unit_open(unit, number)
-                unit_passes(unit, passes)
-            if block_before is not None:
-                out_interleave(*block_before, "scalar")
-            for unit, number, passes in finish:
-                unit_store(unit, "scalar")
-            diff_transpose(2 * j + 2)
-            diff_transpose(2 * j + 3)
-            if block_now is not None:
-                out_transpose(*block_now, 7)
-            for unit, number in open_next:
-                unit_open(unit, number)
-                unit_passes(unit, (Q_PASS,))
+            quantize_even(j)
+            if j == 1:
+                k_quantize(3)
+            quantize_odd(j)
 
         both_j = (J_FIRST, J_SECOND)
-        column4, column5, column6, column7 = [(0, 4, i * P) for i in range(4, 8)]
+        top_left = [(i, 1, 0) for i in range(4)]
         row4, row5, row6, row7 = [(i, 1, 0) for i in range(4, 8)]
+        column4, column5, column6, column7 = [(0, 4, i * P) for i in range(4, 8)]
         corner_a, corner_b = (4, 2, 512), (4, 2, 768)
         corner_c, corner_d = (6, 2, 512), (6, 2, 768)
 
-        finish = [(unit, None, (J_SECOND,)) for unit in top_left[:2]] + [(unit, None, (Q_PASS, J_SECOND)) for unit in top_left[2:]]
-        round_results(4, finish, None, None, [(column4, 1)])
-        round_quantize(4, kr_pair=2, kr_ready=2, finished=top_left)
+        round_scale(3)
+        open_with(top_left[:2], (0, 1), (J_FIRST, Q_PASS))
+        diff_transpose(9)
+        for step in (11, 13, 15):
+            widen_s(step)
+        open_with(top_left[2:], (5, 6), (J_FIRST,))
+        diff_transpose(8)
+        kr_multiply(1)
+        quantize_even(3)
+        kr_quantize(1)
+        quantize_odd(3)
 
-        finish = [(row4, 0, ALL_PASSES), (column4, None, both_j)]
-        round_results(5, finish, None, (0, 0), [(column5, 5), (corner_a, 6)])
-        round_quantize(5, finished=[row4, column4])
+        round_scale(4)
+        go_on_with(top_left[:2], (J_SECOND,))
+        diff_transpose(11)
+        go_on_with(top_left[2:], (Q_PASS, J_SECOND))
+        store_on_scalar(top_left)
+        diff_transpose(10)
+        open_with((column4, column5), (1, 5), (Q_PASS,))
+        kr_multiply(2)
+        quantize_even(4)
+        round_on_scalar(top_left)
+        kr_quantize(2)
+        quantize_odd(4)
+        open_with((corner_a,), (6,), (Q_PASS,))
 
-        finish = [(row5, 4, ALL_PASSES), (column5, None, both_j), (corner_a, None, both_j)]
-        round_results(6, finish, (0, 0), (1, 0), [])
-        round_quantize(6, kr_pair=3, kr_ready=3, out_block=(0, 0), finished=[row5, column5, corner_a])
+        round_scale(5)
+        open_with((row4,), (0,), ALL_PASSES)
+        diff_transpose(13)
+        go_on_with((column4,), both_j)
+        store_on_scalar((row4, column4))
+        diff_transpose(12)
+        out_transpose(0, 0, 7)
+        quantize_even(5)
+        round_on_scalar((row4, column4))
+        quantize_odd(5)
 
-        last = 2 * (ROUNDS - 1)
-        scale(last)
-        for unit, number in ((row6, 0), (column6, 1)):
-            unit_open(unit, number)
-            unit_passes(unit, ALL_PASSES)
+        round_scale(6)
+        open_with((row5,), (0,), ALL_PASSES)
+        go_on_with((column5, corner_a), both_j)
+        diff_transpose(15)
+        out_interleave(0, 0, "scalar")
+        store_on_scalar((row5, column5, corner_a))
+        diff_transpose(14)
+        out_transpose(1, 0, 7)
+        kr_multiply(3)
+        quantize_even(6)
+        round_on_scalar((row5, column5, corner_a))
+        out_quantize(0, 0)
+        kr_quantize(3)
+        quantize_odd(6)
+
+        scale(14)
+        open_with((row6, column6), (1, 0), ALL_PASSES)
         out_interleave(1, 0, "scalar")
-        unit_store(row6, "scalar")
-        unit_store(column6, "scalar")
-        w_quantize(last)
-        wd_quantize(last)
-        scale(last + 1)
-        out_transpose(2, 0, 7)
-        for unit, number in ((column7, 4), (row7, 2)):
-            unit_open(unit, number)
-            unit_passes(unit, (Q_PASS, J_FIRST))
-        w_quantize(last + 1)
-        wd_quantize(last + 1)
+        store_on_scalar((row6, column6))
+        w_quantize(14)
+        wd_quantize(14)
+        scale(15)
+        open_with((column7, row7, corner_b), (3, 2, 5), (Q_PASS, J_FIRST))
+        out_transpose(2, 0, 6)
+        quantize_odd(7)
 
-        unit_passes(column7, (J_SECOND,))
-        unit_passes(row7, (J_SECOND,))
-        unit_open(corner_b, 5)
-        unit_passes(corner_b, ALL_PASSES)
+        go_on_with((column7, row7, corner_b), (J_SECOND,))
         out_quantize(1, 0)
         unit_round(column6, "vector")
         out_interleave(2, 0, "scalar")
         unit_round(row6, "vector")
         unit_store(column7, "scalar")
-        unit_open(corner_c, 6)
-        unit_passes(corner_c, ALL_PASSES)
+        open_with((corner_c,), (6,), ALL_PASSES)
         unit_store(row7, "vector")
-        unit_open(corner_d, 7)
-        unit_passes(corner_d, ALL_PASSES)
+        open_with((corner_d,), (7,), ALL_PASSES)
         unit_round(column7, "vector")
         unit_store(corner_b, "scalar")
         unit_round(row7, "vector")
+        out_quantize(2, 0)
         out_transpose(0, 1, 0)
         out_transpose(1, 1, 1)
-        out_transpose(3, 0, 3)
+        out_transpose(3, 0, 4)
         unit_store(corner_c, "scalar")
         unit_round(corner_b, "vector")
-        out_transpose(2, 1, 4)
+        out_transpose(2, 1, 3)
         unit_store(corner_d, "vector")
-        unit_round(corner_c, "vector")
+        unit_round(corner_c, "scalar")
         out_interleave(0, 1, "scalar")
         unit_round(corner_d, "vector")
         out_transpose(3, 1, 2)
         out_interleave(1, 1, "scalar")
-        out_quantize(2, 0)
         out_interleave(3, 0, "vector")
         out_interleave(2, 1, "scalar")
         out_quantize(0, 1)

from contextlib import ExitStack

import concourse.mybir as mybir
from concourse.masks import make_identity

N, M, L = 1024, 512, 1024
FLOPS = 2 * N * M * L + 2 * N * L * N + 2 * N * M * N

F32 = mybir.dt.float32
BF16 = mybir.dt.bfloat16
U32 = mybir.dt.uint32
I32 = mybir.dt.int32
U8 = mybir.dt.uint8
FP8X4 = mybir.dt.float8_e4m3fn_x4
MULT = mybir.AluOpType.mult
SUB = mybir.AluOpType.subtract
ADD = mybir.AluOpType.add
COPY = mybir.ActivationFunctionType.Copy

P = 128
PACK = 4
HALF = P * PACK
PAIR = 2 * P

STEPS = [(i, h) for h in range(2) for i in range(4)] + [(i, h) for i in range(4, 8) for h in range(2)]

Z_FIRST_ON_VECTOR = slice(0, 384)
Z_FIRST_ON_SCALAR = slice(384, 512)
Z_SECOND_ON_SCALAR = slice(0, 320)
Z_SECOND_ON_VECTOR = slice(320, 512)

J_FIRST, J_SECOND, Q_PASS = 0, 1, 2
ALL_PASSES = (J_FIRST, J_SECOND, Q_PASS)


def summed_in_psum(step):
    return step > 1 and step % 2 == 1


def kz_bank(step):
    return (0, 1, 5, 6)[step % 4]


def diff_bank(step):
    if step % 2 == 0:
        return 2
    return 3 if step % 4 == 1 else 4


def tile_josephkalmanupdate_x1_kernel(tc, s, z, kgain, g, d, r, out_0, out_1, out_2):
    nc = tc.nc
    words_out = out_1.rearrange("h p m t -> h p (m t)").bitcast(I32)
    scales_out = out_2.bitcast(I32)

    with ExitStack() as ctx:
        keep = ctx.enter_context(tc.tile_pool(name="keep", bufs=1))
        work = ctx.enter_context(tc.tile_pool(name="work", bufs=1))
        psum = ctx.enter_context(tc.psum_pool(name="psum", bufs=1))
        ctx.enter_context(tc.manual_schedule())

        def bank(number):
            return psum.tile([P, HALF], F32, name="bank%d" % number, tag="bank%d" % number)

        def kept(name, shape, dtype):
            return keep.tile(shape, dtype, name=name, tag=name, align_bytes=64)

        def rotating(name, shape, dtype, bufs):
            return work.tile(shape, dtype, name=name, tag=name, bufs=bufs, align_bytes=64)

        def handed_over(parity, shape, dtype):
            return rotating("handed_over%d" % (parity % 2), shape, dtype, 1)

        def mx_operand(name):
            return (kept(name + "_codes", [P, N], U32), kept(name + "_scales", [P, N], U8))

        def cols(start, width):
            return slice(start, start + width)

        def quantize(operand, where, values):
            nc.vector.quantize_mx(out=operand[0][:, where].bitcast(FP8X4), scales=operand[1][:, where], in_=values)

        def mx_pass(acc, lhs, lhs_cols, rhs, rhs_cols, start, stop):
            nc.tensor.matmul_mx(
                out=acc,
                lhsT=lhs[0][:, lhs_cols].bitcast(FP8X4),
                lhsT_scale=lhs[1][:, lhs_cols],
                rhs=rhs[0][:, rhs_cols].bitcast(FP8X4),
                rhs_scale=rhs[1][:, rhs_cols],
                start=start,
                stop=stop,
            )

        def copy_on(engine, out, in_):
            if engine == "vector":
                nc.vector.tensor_copy(out=out, in_=in_)
            else:
                nc.scalar.copy(out=out, in_=in_)

        g_sb = kept("g_sb", [P, 2, PACK], BF16)
        d_sb = kept("d_sb", [P, 2, PACK], BF16)
        r_sb = kept("r_sb", [P, PACK], BF16)
        k_raw = [kept("k_raw%d" % c, [P, 2, M], BF16) for c in range(4)]
        s_raw = [[kept("s_raw%d%d" % (a, h), [P, 4, HALF], BF16) for h in range(2)] for a in range(2)]
        z_raw = [kept("z_raw%d" % h, [P, PACK, HALF], BF16) for h in range(2)]

        def load_k(c):
            nc.sync.dma_start(out=k_raw[c][:], in_=kgain[cols(c * PAIR, PAIR), :].rearrange("(e p) m -> p e m", p=P))

        def load_s(a, h):
            rows = s[cols(a * HALF, HALF), cols(h * HALF, HALF)]
            nc.sync.dma_start(out=s_raw[a][h][:], in_=rows.rearrange("(e p) l -> p e l", p=P))

        def load_z(h):
            nc.sync.dma_start(out=z_raw[h][:], in_=z[:, cols(h * HALF, HALF)].rearrange("(p t) l -> p t l", t=PACK))

        load_k(0)
        load_z(0)
        nc.scalar.dma_start(out=g_sb[:], in_=g.rearrange("(h p t) -> p h t", h=2, t=PACK))
        nc.scalar.dma_start(out=d_sb[:], in_=d.rearrange("(h p t) -> p h t", h=2, t=PACK))
        nc.scalar.dma_start(out=r_sb[:], in_=r.rearrange("(p t) -> p t", t=PACK))
        load_k(1)
        load_s(0, 0)
        load_z(1)
        load_s(0, 1)
        load_k(2)
        load_k(3)
        load_s(1, 0)
        load_s(1, 1)

        ident = kept("ident", [P, P], F32)
        make_identity(nc, ident[:])

        kq, krq, zq = mx_operand("kq"), mx_operand("krq"), mx_operand("zq")
        wq = [mx_operand("wq%d" % h) for h in range(2)]
        wdq = [mx_operand("wdq%d" % h) for h in range(2)]
        pass_operands = [(wdq[0], wq[0]), (wdq[1], wq[1]), (krq, kq)]
        factors = kept("factors", [P, 2, 2, PACK], F32)
        out_scales = kept("out_scales", [P, N], U8)
        k_words = [kept("k_words%d" % c, [P, HALF], F32) for c in range(4)]
        kr_values = [kept("kr_values%d" % c, [P, PACK * PAIR], BF16) for c in range(4)]
        z_grouped = [kept("z_grouped0", [P, HALF, PACK], BF16), handed_over(0, [P, HALF, PACK], BF16)]
        kz, neg_kz, s_wide, diff, diff_t, w_values = {}, {}, {}, {}, {}, {}
        unit_acc, unit_done, unit_result = {}, {}, {}
        rounded, out_t, out_values = {}, {}, {}

        def k_transpose(c, number):
            acc = bank(number)
            for e in range(2):
                words = k_raw[c][:, e, :].bitcast(F32)
                for u in range(2):
                    nc.tensor.transpose(acc[:, cols((2 * e + u) * P, P)], words[:, u::2], ident[:])
            nc.scalar.copy(
                out=k_words[c][:].rearrange("p (e n u) -> p e n u", e=2, u=2),
                in_=acc[:].rearrange("p (e u n) -> p e n u", e=2, u=2),
            )

        def k_quantize(c):
            quantize(kq, cols(c * PAIR, PAIR), k_words[c][:].bitcast(BF16))

        def kr_multiply(c):
            nc.vector.tensor_tensor(
                out=kr_values[c][:].rearrange("p (n t) -> p n t", t=PACK),
                in0=k_words[c][:].bitcast(BF16).rearrange("p (n t) -> p n t", t=PACK),
                in1=r_sb[:].unsqueeze(1).to_broadcast([P, PAIR, PACK]),
                op=MULT,
            )

        def kr_quantize(c):
            quantize(krq, cols(c * PAIR, PAIR), kr_values[c][:])

        def z_interleave(h, columns, engine):
            groups = slice(columns.start // 4, columns.stop // 4)
            copy_on(
                engine,
                z_grouped[h][:].rearrange("p (c i) t -> p c t i", i=4)[:, groups],
                z_raw[h][:].rearrange("p t (c i) -> p c t i", i=4)[:, groups],
            )

        def z_quantize(h):
            quantize(zq, cols(h * HALF, HALF), z_grouped[h][:].rearrange("p c t -> p (c t)"))

        def kz_matmul(step):
            i, h = STEPS[step]
            acc = bank(kz_bank(step))
            mx_pass(acc[:], kq, cols(i * P, P), zq, cols(h * HALF, HALF), True, True)
            kz[step] = acc[:].rearrange("n (p t) -> n t p", t=PACK)

        def kz_negate(step):
            neg_kz[step] = kept("neg_kz%d" % step, [P, PACK, P], F32)
            nc.scalar.activation(out=neg_kz[step][:], in_=kz[step], func=COPY, scale=-1.0)

        def s_part(step):
            i, h = STEPS[step]
            return s_raw[i // 4][h][:, i % 4, :].rearrange("n (p t) -> n t p", t=PACK)

        def widen_s(step):
            s_wide[step] = kept("s_wide%d" % step, [P, PACK, P], F32)
            nc.scalar.copy(out=s_wide[step][:], in_=s_part(step))

        def subtract_on_vector(step):
            diff[step] = kept("diff%d" % step, [P, PACK, P], F32)
            nc.vector.tensor_tensor(out=diff[step][:], in0=s_part(step), in1=kz[step], op=SUB)

        def subtract_on_gpsimd(step):
            diff[step] = handed_over(step // 2 - 1, [P, PACK, P], F32)
            for t in (0, 2):
                slots = cols(t, 2)
                nc.gpsimd.tensor_tensor(out=diff[step][:, slots], in0=s_part(step)[:, slots], in1=neg_kz[step][:, slots], op=ADD)

        def diff_transpose(step):
            acc = bank(diff_bank(step))
            for t in range(PACK):
                slot = acc[:, cols(t * P, P)]
                if summed_in_psum(step):
                    nc.tensor.matmul(slot, lhsT=s_wide[step][:, t, :], rhs=ident[:], is_transpose=True, start=True, stop=False)
                    nc.tensor.matmul(slot, lhsT=neg_kz[step][:, t, :], rhs=ident[:], is_transpose=True, start=False, stop=True)
                else:
                    nc.tensor.transpose(slot, diff[step][:, t, :], ident[:])
            diff_t[step] = acc

        def scale(step):
            h = STEPS[step][1]
            shape = [P, 2, P, PACK]
            if step % 2 == 1:
                w_values[step] = handed_over(step // 2 + 1, shape, BF16)
            else:
                w_values[step] = rotating("w_values", shape, BF16, 2)
            nc.vector.tensor_tensor(
                out=w_values[step][:],
                in0=diff_t[step][:].rearrange("p (t n) -> p n t", t=PACK).unsqueeze(1).to_broadcast(shape),
                in1=factors[:, h].unsqueeze(2).to_broadcast(shape),
                op=MULT,
            )

        def w_quantize(step):
            i, h = STEPS[step]
            quantize(wq[h], cols(i * P, P), w_values[step][:, 0].rearrange("p n t -> p (n t)"))

        def wd_quantize(step):
            i, h = STEPS[step]
            quantize(wdq[h], cols(i * P, P), w_values[step][:, 1].rearrange("p n t -> p (n t)"))

        def unit_open(unit, number):
            unit_acc[unit] = bank(number)
            unit_done[unit] = 0

        def unit_passes(unit, passes):
            first, count, col = unit
            width = HALF // count
            for k in passes:
                lhs, rhs = pass_operands[k]
                for e in range(count):
                    unit_done[unit] = unit_done[unit] + 1
                    mx_pass(
                        unit_acc[unit][:, cols(e * width, width)], lhs, cols((first + e) * P, P), rhs, cols(col, width),
                        unit_done[unit] == 1, unit_done[unit] == len(ALL_PASSES) * count,
                    )

        def unit_store(unit, engine):
            first, count, col = unit
            unit_result[unit] = rotating("result", [P, HALF], F32, 10)
            copy_on(engine, unit_result[unit][:], unit_acc[unit][:])
            nc.sync.dma_start(
                out=out_0[cols(first * P, count * P), cols(col, HALF // count)].rearrange("(e n) m -> n e m", e=count),
                in_=unit_result[unit][:].rearrange("n (e m) -> n e m", e=count),
            )

        def unit_round(unit, engine):
            first, count, col = unit
            h, partitions = col // HALF, cols((col % HALF) // PACK, P // count)
            src = unit_result[unit][:].rearrange("n (e p u v) -> n e u p v", e=count, u=2, v=2)
            tiles = min(count, 2)
            for e in range(0, count, tiles):
                c = (first + e) // 2
                if (c, h) not in rounded:
                    rounded[c, h] = kept("rounded%d%d" % (c, h), [P, 2, 2, P, 2], BF16)
                copy_on(engine, rounded[c, h][:, cols((first + e) % 2, tiles), :, partitions, :], src[:, cols(e, tiles)])

        def out_transpose(c, h, number):
            out_t[c, h] = bank(number)
            words = rounded[c, h][:].rearrange("n e u p v -> n (e u p v)").bitcast(F32)
            for j in range(4):
                nc.tensor.transpose(out_t[c, h][:, cols(j * P, P)], words[:, cols(j * P, P)], ident[:])

        def out_interleave(c, h, engine):
            out_values[c, h] = rotating("out_values", [P, HALF], F32, 5)
            copy_on(
                engine,
                out_values[c, h][:].rearrange("p (e n u) -> p e n u", e=2, u=2),
                out_t[c, h][:].rearrange("p (e u n) -> p e n u", e=2, u=2),
            )

        def out_quantize(c, h):
            codes = kept("out_codes%d%d" % (c, h), [P, PAIR], U32)
            nc.vector.quantize_mx(
                out=codes[:].bitcast(FP8X4),
                scales=out_scales[4 * h :, cols(c * PAIR, PAIR)],
                in_=out_values[c, h][:].bitcast(BF16),
            )
            nc.sync.dma_start(out=words_out[h, :, cols(c * PAIR, PAIR)], in_=codes[:].bitcast(I32))

        k_transpose(0, 7)
        z_interleave(0, Z_FIRST_ON_VECTOR, "vector")
        z_interleave(0, Z_FIRST_ON_SCALAR, "scalar")
        k_quantize(0)
        k_transpose(1, 2)
        z_quantize(0)
        kz_matmul(0)
        kz_matmul(1)
        kr_multiply(0)
        k_quantize(1)
        kz_matmul(2)
        kz_matmul(3)
        z_interleave(1, Z_SECOND_ON_SCALAR, "scalar")
        subtract_on_vector(0)
        subtract_on_vector(1)
        diff_transpose(0)
        diff_transpose(1)
        widen_s(3)
        kz_negate(2)
        kz_negate(3)
        k_transpose(2, 7)
        nc.vector.tensor_copy(out=factors[:, :, 0, :], in_=g_sb[:])
        nc.vector.tensor_tensor(out=factors[:, :, 1, :], in0=g_sb[:], in1=d_sb[:], op=MULT)
        z_interleave(1, Z_SECOND_ON_VECTOR, "vector")
        z_quantize(1)

        def round_scale(j):
            subtract_on_gpsimd(2 * j + 2)
            scale(2 * j)
            scale(2 * j + 1)

        def quantize_even(j):
            wd_quantize(2 * j)
            w_quantize(2 * j)

        def quantize_odd(j):
            w_quantize(2 * j + 1)
            wd_quantize(2 * j + 1)

        def open_with(units, numbers, passes):
            for unit, number in zip(units, numbers):
                unit_open(unit, number)
                unit_passes(unit, passes)

        def go_on_with(units, passes):
            for unit in units:
                unit_passes(unit, passes)

        def store_on_scalar(units):
            for unit in units:
                unit_store(unit, "scalar")

        def round_on_scalar(units):
            for unit in units:
                unit_round(unit, "scalar")

        round_scale(0)
        kz_matmul(4)
        kz_matmul(5)
        k_transpose(3, 4)
        kz_matmul(6)
        kz_matmul(7)
        kz_negate(4)
        kz_negate(5)
        widen_s(5)
        kz_negate(6)
        kz_negate(7)
        diff_transpose(2)
        diff_transpose(3)
        quantize_even(0)
        k_quantize(2)
        kr_quantize(0)
        quantize_odd(0)

        for j in (1, 2):
            ahead = range(4 * j + 4, 4 * j + 8)
            round_scale(j)
            kz_matmul(ahead[0])
            kz_matmul(ahead[1])
            diff_transpose(2 * j + 3)
            kz_matmul(ahead[2])
            kz_matmul(ahead[3])
            widen_s(2 * j + 5)
            for step in ahead:
                kz_negate(step)
            diff_transpose(2 * j + 2)
            quantize_even(j)
            if j == 1:
                k_quantize(3)
            quantize_odd(j)

        both_j = (J_FIRST, J_SECOND)
        top_left = [(i, 1, 0) for i in range(4)]
        row4, row5, row6, row7 = [(i, 1, 0) for i in range(4, 8)]
        column4, column5, column6, column7 = [(0, 4, i * P) for i in range(4, 8)]
        corner_a, corner_b = (4, 2, 512), (4, 2, 768)
        corner_c, corner_d = (6, 2, 512), (6, 2, 768)

        round_scale(3)
        open_with(top_left[:2], (0, 1), (J_FIRST, Q_PASS))
        diff_transpose(9)
        for step in (11, 13, 15):
            widen_s(step)
        open_with(top_left[2:], (5, 6), (J_FIRST,))
        diff_transpose(8)
        kr_multiply(1)
        quantize_even(3)
        kr_quantize(1)
        quantize_odd(3)

        round_scale(4)
        go_on_with(top_left[:2], (J_SECOND,))
        diff_transpose(11)
        go_on_with(top_left[2:], (Q_PASS, J_SECOND))
        store_on_scalar(top_left)
        diff_transpose(10)
        open_with((column4, column5), (1, 5), (Q_PASS,))
        kr_multiply(2)
        quantize_even(4)
        round_on_scalar(top_left)
        kr_quantize(2)
        quantize_odd(4)
        open_with((corner_a,), (6,), (Q_PASS,))

        round_scale(5)
        open_with((row4,), (0,), ALL_PASSES)
        diff_transpose(13)
        go_on_with((column4,), both_j)
        store_on_scalar((row4, column4))
        diff_transpose(12)
        out_transpose(0, 0, 7)
        quantize_even(5)
        round_on_scalar((row4, column4))
        quantize_odd(5)

        round_scale(6)
        open_with((row5,), (0,), ALL_PASSES)
        go_on_with((column5, corner_a), both_j)
        diff_transpose(15)
        out_interleave(0, 0, "scalar")
        store_on_scalar((row5, column5, corner_a))
        diff_transpose(14)
        out_transpose(1, 0, 7)
        kr_multiply(3)
        quantize_even(6)
        round_on_scalar((row5, column5, corner_a))
        out_quantize(0, 0)
        kr_quantize(3)
        quantize_odd(6)

        scale(14)
        open_with((row6, column6), (1, 0), ALL_PASSES)
        out_interleave(1, 0, "scalar")
        store_on_scalar((row6, column6))
        w_quantize(14)
        wd_quantize(14)
        scale(15)
        open_with((column7, row7, corner_b), (3, 2, 5), (Q_PASS, J_FIRST))
        out_transpose(2, 0, 6)
        quantize_odd(7)

        go_on_with((column7, row7, corner_b), (J_SECOND,))
        out_quantize(1, 0)
        unit_round(column6, "vector")
        out_interleave(2, 0, "scalar")
        unit_round(row6, "vector")
        unit_store(column7, "scalar")
        open_with((corner_c,), (6,), ALL_PASSES)
        unit_store(row7, "vector")
        open_with((corner_d,), (7,), ALL_PASSES)
        unit_round(column7, "vector")
        unit_store(corner_b, "scalar")
        unit_round(row7, "vector")
        out_quantize(2, 0)
        out_transpose(0, 1, 0)
        out_transpose(1, 1, 1)
        out_transpose(3, 0, 4)
        unit_store(corner_c, "scalar")
        unit_round(corner_b, "vector")
        out_transpose(2, 1, 3)
        unit_store(corner_d, "vector")
        unit_round(corner_c, "scalar")
        out_interleave(0, 1, "scalar")
        unit_round(corner_d, "vector")
        out_transpose(3, 1, 2)
        out_interleave(1, 1, "scalar")
        out_interleave(3, 0, "vector")
        out_interleave(2, 1, "scalar")
        out_quantize(0, 1)
        out_quantize(1, 1)
        out_interleave(3, 1, "scalar")
        out_quantize(3, 0)
        out_quantize(2, 1)
        out_quantize(3, 1)

        for quad in range(4):
            queue = nc.sync if quad % 2 == 0 else nc.scalar
            queue.dma_start(out=scales_out[:, cols(4 * quad, 4), :], in_=out_scales[cols(32 * quad, 8), :].bitcast(I32))
